import numpy as np
import ml_dtypes


def mxq(x, axis, fmt="e4m3"):
    dtype, down = {"e4m3": (ml_dtypes.float8_e4m3fn, 7), "e5m2": (ml_dtypes.float8_e5m2, 14)}[fmt]
    v = np.moveaxis(np.asarray(x, np.float32).astype(ml_dtypes.bfloat16).astype(np.float64), axis, -1)
    blocks = v.reshape(v.shape[:-1] + (-1, 32))
    amax = np.abs(blocks).max(-1, keepdims=True)
    byte = np.maximum(np.where(amax > 0, np.frexp(amax)[1] - 1 + 127, 0) - down, 1)
    scale = np.exp2(byte - 127.0)
    codes = (blocks / scale).astype(np.float32).astype(dtype).astype(np.float64)
    return np.moveaxis((codes * scale).reshape(v.shape), -1, axis)


WIDE = False


def mx_kscale(k):
    if not WIDE:
        return np.ones(k)
    levels = np.array([10, -10, 5, -5, 0])
    if k % 512:
        return np.exp2(np.random.permutation(np.resize(levels, k // 32))).repeat(32)
    a = np.empty((k // 512, 16))
    for p in range(k // 512):
        a[p, :8] = np.random.permutation(np.resize(levels, 8))
        for g in range(8):
            far = levels[np.abs(levels - a[p, g]) >= 10]
            a[p, g + 8] = far[np.random.randint(len(far))]
    return np.exp2(a.ravel()).repeat(32)


BF16 = ml_dtypes.bfloat16


def bf(x):
    return np.asarray(x, np.float32).astype(BF16)


def f64(x):
    return np.asarray(x).astype(np.float64)


N, K, M = 4096, 1024, 512
RADIUS = 64.0


def smoothed_vertex(grad):
    v = -2.0 * grad
    ex = np.exp(v - v.max(-1, keepdims=True))
    return RADIUS * (ex / ex.sum(-1, keepdims=True))


def draw0():
    s, t = mx_kscale(M), mx_kscale(K)
    r = bf(0.5 * np.random.standard_normal((N, M)))
    p = 1.0 + 0.1 * np.random.standard_normal(M)
    enc = np.random.standard_normal((M, K)) * 2.0 / np.sqrt(M)
    g = 1.0 + 0.1 * np.random.standard_normal(K)
    dec = np.random.standard_normal((K, M)) * 0.045 * (K / M) ** 0.25
    grad = (f64(r) * p[None, :]) @ enc
    far = np.random.uniform(size=(N, 1)) < 0.125
    z = np.where(far, 400.0 / K * np.maximum(-grad, 0.0), np.random.uniform(0.0, 2.0 * RADIUS / K, (N, K)))
    return {"r": r, "z": bf(z), "p": bf(p * s), "enc": bf(enc / s[:, None]), "g": bf(g * t), "dec": bf(dec / t[:, None])}


def core(r, z, p, enc, g, dec):
    m, k = enc.shape
    r, z, p, g = f64(r), f64(z), f64(p), f64(g)
    grad = mxq(r * p[None, :], 1, "e4m3") @ mxq(f64(enc), 0, "e4m3")
    s = smoothed_vertex(grad)
    d = s - z
    e = mxq(d * g[None, :], 1, "e4m3") @ mxq(f64(dec), 0, "e4m3")
    gap = -np.sum(grad * d, axis=-1) / np.sqrt(m * k)
    curv = np.mean(e * e, axis=-1) + 1e-6
    gamma = np.minimum(np.maximum(gap / curv, 0.0), 1.0)
    return r + gamma[:, None] * e


def e4m3fn_bytes(y):
    return np.clip(np.asarray(y, np.float64), -448.0, 448.0).astype(np.float32).astype(ml_dtypes.float8_e4m3fn).view(np.uint8)


def e4m3fn_values(b):
    return np.asarray(b, np.uint8).view(ml_dtypes.float8_e4m3fn).astype(np.float64)


def setup_inputs():
    d = draw0()
    x0 = np.asarray(d['enc']).astype(np.float64)
    s = (np.max(np.abs(x0), axis=(1,), keepdims=True) / 448.0).astype(np.float32)
    out = {}
    for k, v in d.items():
        if k == 'enc':
            out['enc_bytes'] = e4m3fn_bytes(x0 / s.astype(np.float64))
            out['enc_scale'] = s
        else:
            out[k] = v
    return out


def reference(r, z, p, enc_bytes, enc_scale, g, dec):
    return core(r, z, p, e4m3fn_values(enc_bytes) * enc_scale.astype(np.float64), g, dec)

@@ -1,0 +1,375 @@
+import math
+from contextlib import ExitStack
+
+import concourse.mybir as mybir
+from concourse.masks import make_identity
+
+ROWS, CODES, FEATS = 4096, 1024, 512
+RADIUS = 64.0
+FLOPS = 2 * 2 * ROWS * CODES * FEATS
+
+F32 = mybir.dt.float32
+BF16 = mybir.dt.bfloat16
+U32 = mybir.dt.uint32
+U8 = mybir.dt.uint8
+FP8 = mybir.dt.float8_e4m3fn
+FP8X4 = mybir.dt.float8_e4m3fn_x4
+ALU = mybir.AluOpType
+ACT = mybir.ActivationFunctionType
+
+P = 128
+GROUP = 4
+NT = ROWS // P
+NPAIR = NT // 2
+NGROUP = NT // GROUP
+HALF = 512
+K1 = -math.sqrt(FEATS * CODES) / FEATS
+K2 = -math.sqrt(FEATS * CODES) * 1e-6
+
+PLAN = [
+    ("row_min", 0, 0),
+    ("scale_step", -6, None),
+    ("grad", 0, 1),
+    ("d_gain", -2, 0),
+    ("d_transpose", -2, 1),
+    ("subtract", -1, 1),
+    ("square", -3, None),
+    ("decode", -4, None),
+    ("row_min", 0, 1),
+    ("gap", -1, 0),
+    ("exponent", 0, 0),
+    ("finish", -8, None),
+    ("d_gain", -2, 1),
+    ("exponent", 0, 1),
+    ("grad", 1, 0),
+    ("gap", -1, 1),
+    ("total_a", 0, None),
+    ("total_b", 0, None),
+    ("square", -4, None),
+    ("finish", -5, None),
+    ("recip_total", 0, None),
+    ("row_min", 1, 0),
+    ("grad", 1, 1),
+    ("normalise", 0, 0),
+    ("d_transpose", -1, 0),
+    ("d_transpose", -1, 1),
+    ("curvature", -2, None),
+    ("normalise", 0, 1),
+    ("r_quant", 1, None),
+    ("row_min", 1, 1),
+    ("subtract", 0, 0),
+    ("d_gain", -1, 0),
+    ("exponent", 1, 0),
+    ("recip_curv", -2, None),
+    ("d_gain", -1, 1),
+    ("subtract", 0, 1),
+    ("r_transpose", 2, None),
+    ("exponent", 1, 1),
+    ("gap_sum", -1, None),
+    ("gap", 0, 0),
+    ("total_a", 1, None),
+    ("ratio_a", -2, None),
+    ("ratio_b", -2, None),
+    ("total_b", 1, None),
+    ("clip", -2, None),
+    ("step", -2, None),
+    ("recip_total", 1, None),
+    ("r_gain", 2, None),
+    ("grad", 2, 0),
+    ("normalise", 1, 0),
+    ("d_transpose", 0, 0),
+    ("d_quant", -1, None),
+    ("scale_step", -3, None),
+    ("gap", 0, 1),
+    ("subtract", 1, 0),
+    ("normalise", 1, 1),
+    ("decode", -1, None),
+]
+FILL = {("gap", -1, 0): 0, ("gap", -1, 1): 1, ("d_gain", -1, 0): 2, ("d_gain", -1, 1): 3}
+
+
+def tile_smoothedfrankwolfesimplexcoding_t_kernel(tc, r, z, p, enc_bytes, enc_scale, g, dec, out):
+    nc = tc.nc
+    r_hbm = r.rearrange("(g p j) m -> g p j m", p=P, j=GROUP)
+    z_hbm = z.rearrange("(g p j) k -> g p j k", p=P, j=GROUP)
+    out_hbm = out.rearrange("(g p j) m -> g p j m", p=P, j=GROUP)
+
+    with ExitStack() as ctx:
+        keep = ctx.enter_context(tc.tile_pool(name="keep", bufs=1))
+        pool = ctx.enter_context(tc.tile_pool(name="work", bufs=2))
+        psum = ctx.enter_context(tc.psum_pool(name="psum", bufs=2))
+        ctx.enter_context(tc.manual_schedule())
+
+        ident = keep.tile([P, P], F32, name="ident")
+        warm = keep.tile([P, 2], F32, name="warm")
+        enc_u8 = keep.tile([P, 4, CODES], U8, name="enc_u8", align_bytes=64)
+        enc_s = keep.tile([P, 4], F32, name="enc_s")
+        p_sb = keep.tile([P, 4], BF16, name="p_sb")
+        g_sb = keep.tile([P, 2, 4], BF16, name="g_sb")
+        enc_wide = keep.tile([P, 4, CODES], BF16, name="enc_wide", align_bytes=64)
+        enc_grp = keep.tile([P, 2, 4, P, 4], BF16, name="enc_grp", align_bytes=64)
+        enc_codes = keep.tile([P, CODES], U32, name="enc_codes", align_bytes=64)
+        enc_scales = keep.tile([P, CODES], U8, name="enc_scales", align_bytes=64)
+        dec_raw = keep.tile([P, 2, 4, FEATS], BF16, name="dec_raw", align_bytes=64)
+        dec_grp = keep.tile([P, 2, FEATS, 4], BF16, name="dec_grp", align_bytes=64)
+        dec_codes = keep.tile([P, 2, FEATS], U32, name="dec_codes", align_bytes=64)
+        dec_scales = keep.tile([P, 2, FEATS], U8, name="dec_scales", align_bytes=64)
+
+        st = {}
+
+        def load_r(k):
+            t = pool.tile([P, GROUP, FEATS], BF16, name="r_sb", tag="r_sb", bufs=6, align_bytes=64)
+            nc.sync.dma_start(out=t[:], in_=r_hbm[k])
+            st["r", k] = t
+
+        def load_z(k):
+            t = pool.tile([P, GROUP, CODES], BF16, name="z_sb", tag="z_sb", bufs=3, align_bytes=64)
+            nc.sync.dma_start(out=t[:], in_=z_hbm[k])
+            st["z", k] = t
+
+        def r_transpose(j):
+            t = psum.tile([P, 2, 2 * P], F32, name="t_ps", tag="t_ps", bufs=2)
+            for i in range(2):
+                n = 2 * j + i
+                words = st["r", n // GROUP][:, n % GROUP, :].bitcast(F32)
+                for u in range(2):
+                    nc.tensor.transpose(t[:, u, i * P : (i + 1) * P], words[:, u : 2 * P : 2], ident[:])
+            st["rt", j] = t
+
+        def r_gain(j):
+            t = pool.tile([P, 2 * P * 4], BF16, name="rp_b", tag="rp_b", bufs=2, align_bytes=64)
+            nc.vector.tensor_tensor(
+                out=t[:].rearrange("p (w u e) -> p w u e", u=2, e=2),
+                in0=st.pop(("rt", j))[:].bitcast(BF16).rearrange("p u (w e) -> p w u e", e=2),
+                in1=p_sb[:].unsqueeze(1).broadcast_to([P, 2 * P, 4]).rearrange("p w (u e) -> p w u e", e=2),
+                op=ALU.mult,
+            )
+            st["rp", j] = t
+
+        def r_quant(j):
+            c = pool.tile([P, 2 * P], U32, name="rp_codes", tag="rp_codes", bufs=4, align_bytes=64)
+            s = pool.tile([P, 2 * P], U8, name="rp_scales", tag="rp_scales", bufs=4, align_bytes=64)
+            nc.vector.quantize_mx(out=c[:].bitcast(FP8X4), scales=s[:], in_=st.pop(("rp", j))[:])
+            st["rq", j] = (c, s)
+
+        def grad(n, q):
+            c, s = st["rq", n // 2]
+            cols = slice((n % 2) * P, (n % 2 + 1) * P)
+            t = psum.tile([P, HALF], F32, name="grad", tag="grad", bufs=4)
+            h = slice(q * HALF, (q + 1) * HALF)
+            nc.tensor.matmul_mx(
+                out=t[:], lhsT=c[:, cols].bitcast(FP8X4), lhsT_scale=s[:, cols],
+                rhs=enc_codes[:, h].bitcast(FP8X4), rhs_scale=enc_scales[:, h], start=True, stop=True,
+            )
+            st["grad", n, q] = t
+
+        def row_min(n, q):
+            junk = pool.tile([P, HALF], F32, name="v_junk", tag="v_junk", bufs=4)
+            m = pool.tile([P, 1], F32, name="row_min", tag="row_min", bufs=6)
+            nc.vector.tensor_scalar(
+                out=junk[:], in0=st["grad", n, q][:], scalar1=2.0, scalar2=None if q == 0 else st["min", n][:],
+                op0=ALU.mult, op1=ALU.min, accum_out=m[:],
+            )
+            st["min", n] = m
+
+        def exponent(n, q):
+            if q == 0:
+                st["s", n] = pool.tile([P, 2, 4, P], F32, name="s_sb", tag="s_sb", bufs=3)
+                st["sums", n] = pool.tile([P, 2], F32, name="sums", tag="sums", bufs=4)
+            nc.scalar.activation(
+                out=st["s", n][:, q].rearrange("p t c -> p (t c)"), in_=st["grad", n, q][:], func=ACT.Exp,
+                scale=-2.0, bias=st["min", n][:], accum_out=st["sums", n][:, q : q + 1],
+            )
+
+        def total_a(n):
+            a = pool.tile([P, 1], F32, name="sum_a", tag="sum_a", bufs=4)
+            nc.scalar.activation(out=a[:], in_=st["sums", n][:, 0:1], func=ACT.Copy, scale=1.0 / RADIUS)
+            st["sum_a", n] = a
+
+        def total_b(n):
+            b = pool.tile([P, 1], F32, name="sum_b", tag="sum_b", bufs=4)
+            nc.scalar.activation(out=b[:], in_=st["sums", n][:, 1:2], func=ACT.Identity, scale=1.0 / RADIUS, bias=st["sum_a", n][:])
+            st["tot", n] = b
+
+        def recip_total(n):
+            c = pool.tile([P, 1], F32, name="coef", tag="coef", bufs=4)
+            nc.vector.reciprocal(out=c[:], in_=st.pop(("tot", n))[:])
+            st["coef", n] = c
+
+        def normalise(n, q):
+            s = st["s", n][:, q].rearrange("p t c -> p (t c)")
+            nc.scalar.activation(out=s, in_=s, func=ACT.Copy, scale=st["coef", n][:])
+
+        def subtract(n, q):
+            if q == 0:
+                st["d", n] = pool.tile([P, 2, 4, P], F32, name="d_sb", tag="d_sb", bufs=3)
+            zt = st["z", n // GROUP][:, n % GROUP, q * HALF : (q + 1) * HALF].rearrange("p (c t) -> p t c", t=4)
+            nc.gpsimd.tensor_tensor(out=st["d", n][:, q], in0=st["s", n][:, q], in1=zt, op=ALU.subtract)
+
+        def gap(n, q):
+            if ("gaps", n // 2) not in st:
+                st["gaps", n // 2] = pool.tile([P, 2, 2], F32, name="gaps", tag="gaps", bufs=4)
+            junk = pool.tile([P, HALF], F32, name="v_junk", tag="v_junk", bufs=4)
+            nc.vector.scalar_tensor_tensor(
+                out=junk[:], in0=st["grad", n, q][:], scalar=1.0, in1=st["d", n][:, q].rearrange("p t c -> p (t c)"),
+                op0=ALU.mult, op1=ALU.mult, accum_out=st["gaps", n // 2][:, n % 2, q : q + 1],
+            )
+
+        def d_transpose(n, q):
+            t = psum.tile([P, 4, P], F32, name="t_ps", tag="t_ps", bufs=2)
+            for i in range(4):
+                nc.tensor.transpose(t[:, i, :], st["d", n][:, q, i, :], ident[:])
+            st["dt", n, q] = t
+
+        def d_gain(n, q):
+            if ("dg", n // 2) not in st:
+                st["dg", n // 2] = pool.tile([P, 2, 2, P, 4], BF16, name="dg_b", tag="dg_b", bufs=2, align_bytes=64)
+            nc.vector.tensor_tensor(
+                out=st["dg", n // 2][:, n % 2, q], in0=st.pop(("dt", n, q))[:].rearrange("p t w -> p w t"),
+                in1=g_sb[:, q, :].unsqueeze(1).broadcast_to([P, P, 4]), op=ALU.mult,
+            )
+
+        def d_quant(j):
+            c = pool.tile([P, 4 * P], U32, name="d_codes", tag="d_codes", bufs=2, align_bytes=64)
+            s = pool.tile([P, 4 * P], U8, name="d_scales", tag="d_scales", bufs=2, align_bytes=64)
+            nc.vector.quantize_mx(out=c[:].bitcast(FP8X4), scales=s[:], in_=st["dg", j][:].rearrange("p i q w t -> p (i q w t)"))
+            st["dq", j] = (c, s)
+
+        def decode(n):
+            c, s = st["dq", n // 2]
+            t = psum.tile([P, FEATS], F32, name="e_ps", tag="e_ps", bufs=2)
+            for q in range(2):
+                cols = slice(((n % 2) * 2 + q) * P, ((n % 2) * 2 + q + 1) * P)
+                nc.tensor.matmul_mx(
+                    out=t[:], lhsT=c[:, cols].bitcast(FP8X4), lhsT_scale=s[:, cols],
+                    rhs=dec_codes[:, q, :].bitcast(FP8X4), rhs_scale=dec_scales[:, q, :], start=(q == 0), stop=(q == 1),
+                )
+            st["e", n] = t
+
+        def square(n):
+            if ("esq", n // 2) not in st:
+                st["esq", n // 2] = pool.tile([P, 2], F32, name="esq", tag="esq", bufs=2)
+            junk = pool.tile([P, FEATS], BF16, name="s_junk", tag="s_junk", bufs=2)
+            nc.scalar.activation(out=junk[:], in_=st["e", n][:], func=ACT.Square, accum_out=st["esq", n // 2][:, n % 2 : n % 2 + 1])
+
+        def curvature(j):
+            t = pool.tile([P, 2], F32, name="den", tag="den", bufs=2)
+            nc.scalar.activation(out=t[:], in_=st["esq", j][:], func=ACT.Copy, scale=K1, bias=K2)
+            st["den", j] = t
+
+        def recip_curv(j):
+            t = pool.tile([P, 2], F32, name="rden", tag="rden", bufs=3)
+            nc.vector.reciprocal(out=t[:], in_=st.pop(("den", j))[:])
+            st["rden", j] = t
+
+        def gap_sum(j):
+            u = pool.tile([P, 2], F32, name="gsum", tag="gsum", bufs=4)
+            nc.vector.tensor_reduce(out=u[:], in_=st["gaps", j][:], axis=mybir.AxisListType.X, op=ALU.add)
+            st["gsum", j] = u
+
+        def ratio(j, i):
+            if ("gam_a", j) not in st:
+                st["gam_a", j] = pool.tile([P, 2], F32, name="gam_a", tag="gam_a", bufs=2)
+            a = st["gam_a", j]
+            nc.scalar.activation(out=a[:, i : i + 1], in_=st["gsum", j][:, i : i + 1], func=ACT.Relu, scale=st["rden", j][:, i : i + 1])
+
+        def ratio_a(j):
+            ratio(j, 0)
+
+        def ratio_b(j):
+            ratio(j, 1)
+
+        def clip(j):
+            b = pool.tile([P, 2], F32, name="gam_b", tag="gam_b", bufs=2)
+            nc.scalar.activation(out=b[:], in_=st["gam_a", j][:], func=ACT.Relu, scale=-1.0, bias=1.0)
+            st["gam_b", j] = b
+
+        def step(j):
+            c = pool.tile([P, 2], F32, name="gam_c", tag="gam_c", bufs=3)
+            nc.scalar.activation(out=c[:], in_=st["gam_b", j][:], func=ACT.Copy, scale=-1.0, bias=1.0)
+            st["gam", j] = c
+
+        def scale_step(n):
+            t = pool.tile([P, FEATS], F32, name="ge", tag="ge", bufs=4)
+            nc.scalar.activation(out=t[:], in_=st.pop(("e", n))[:], func=ACT.Copy, scale=st["gam", n // 2][:, n % 2 : n % 2 + 1])
+            st["ge", n] = t
+
+        def finish(n):
+            t = pool.tile([P, FEATS], F32, name="o_sb", tag="o_sb", bufs=4)
+            nc.gpsimd.tensor_tensor(out=t[:], in0=st.pop(("ge", n))[:], in1=st["r", n // GROUP][:, n % GROUP, :], op=ALU.add)
+            nc.sync.dma_start(out=out_hbm[n // GROUP][:, n % GROUP, :], in_=t[:])
+
+        def widen(q):
+            h = slice(q * HALF, (q + 1) * HALF)
+            for t in (1, 2, 3):
+                nc.scalar.activation(out=enc_wide[:, t, h], in_=enc_u8[:, t, h].bitcast(FP8), func=ACT.Copy, scale=enc_s[:, t : t + 1])
+            nc.vector.tensor_scalar(out=enc_wide[:, 0, h], in0=enc_u8[:, 0, h].bitcast(FP8), scalar1=enc_s[:, 0:1], scalar2=None, op0=ALU.mult)
+
+        def enc_interleave(q):
+            h = slice(q * HALF, (q + 1) * HALF)
+            nc.vector.tensor_copy(out=enc_grp[:, q], in_=enc_wide[:, :, h].rearrange("p t (c u) -> p u c t", u=4))
+
+        def enc_quant(q):
+            h = slice(q * HALF, (q + 1) * HALF)
+            nc.vector.quantize_mx(out=enc_codes[:, h].bitcast(FP8X4), scales=enc_scales[:, h], in_=enc_grp[:, q].rearrange("p u c t -> p (u c t)"))
+
+        def dec_piece(i):
+            q, m = i // 2, slice((i % 2) * 256, (i % 2 + 1) * 256)
+            nc.vector.tensor_copy(out=dec_grp[:, q, m, :], in_=dec_raw[:, q, :, m].rearrange("p t m -> p m t"))
+
+        def dec_quant(q):
+            nc.vector.quantize_mx(out=dec_codes[:, q, :].bitcast(FP8X4), scales=dec_scales[:, q, :], in_=dec_grp[:, q].rearrange("p m t -> p (m t)"))
+
+        nc.sync.dma_start(out=enc_u8[:], in_=enc_bytes.rearrange("(p t) k -> p t k", t=4))
+        nc.scalar.dma_start(out=enc_s[:], in_=enc_scale.rearrange("(p t) o -> p (t o)", t=4))
+        nc.scalar.dma_start(out=p_sb[:], in_=p.rearrange("(p t) -> p t", t=4))
+        nc.scalar.dma_start(out=g_sb[:], in_=g.rearrange("(q p t) -> p q t", p=P, t=4))
+        load_r(0)
+        load_z(0)
+        nc.sync.dma_start(out=dec_raw[:], in_=dec.rearrange("(q p t) m -> p q t m", p=P, t=4))
+        load_r(1)
+        load_z(1)
+        nc.vector.memset(warm[:], 0.0)
+        nc.scalar.activation(out=warm[:, 1:2], in_=warm[:, 0:1], func=ACT.Exp)
+        make_identity(nc, ident[:])
+
+        stages = {
+            "r_transpose": r_transpose, "r_gain": r_gain, "r_quant": r_quant, "grad": grad, "row_min": row_min, "exponent": exponent,
+            "total_a": total_a, "total_b": total_b, "recip_total": recip_total, "normalise": normalise, "subtract": subtract, "gap": gap,
+            "d_transpose": d_transpose, "d_gain": d_gain, "d_quant": d_quant, "decode": decode, "square": square, "curvature": curvature,
+            "recip_curv": recip_curv, "gap_sum": gap_sum, "ratio_a": ratio_a, "ratio_b": ratio_b, "clip": clip, "step": step,
+            "scale_step": scale_step, "finish": finish,
+        }
+        by_pair = {"r_transpose", "r_gain", "r_quant", "d_quant", "curvature", "recip_curv", "gap_sum", "ratio_a", "ratio_b", "clip", "step"}
+
+        def period(k):
+            if k > 0 and k % 2 == 0 and k // 2 + 1 < NGROUP:
+                load_r(k // 2 + 1)
+                load_z(k // 2 + 1)
+            for name, off, q in PLAN:
+                if name in by_pair:
+                    if 0 <= k + off < NPAIR:
+                        stages[name](k + off)
+                    elif name == "d_quant" and k + off == -1:
+                        dec_quant(0)
+                        dec_quant(1)
+                else:
+                    n = 2 * k + off
+                    if (name, n, q) in FILL:
+                        dec_piece(FILL[name, n, q])
+                    if 0 <= n < NT:
+                        if q is None:
+                            stages[name](n)
+                        else:
+                            stages[name](n, q)
+
+        widen(0)
+        widen(1)
+        period(-2)
+        enc_interleave(0)
+        enc_quant(0)
+        period(-1)
+        enc_interleave(1)
+        enc_quant(1)
+        for k in range(NPAIR + 5):
+            period(k)

@@ -25,67 +25,71 @@ NGROUP = NT // GROUP
 HALF = 512
 K1 = -math.sqrt(FEATS * CODES) / FEATS
 K2 = -math.sqrt(FEATS * CODES) * 1e-6
-
+VFIN = 4
 PLAN = [
     ("row_min", 0, 0),
-    ("scale_step", -6, None),
     ("grad", 0, 1),
+    ("clip", -5, None),
+    ("step", -5, None),
     ("d_gain", -2, 0),
-    ("d_transpose", -2, 1),
-    ("subtract", -1, 1),
-    ("square", -3, None),
+    ("scale_step", -5, None),
     ("decode", -4, None),
+    ("subtract", -1, 1),
     ("row_min", 0, 1),
     ("gap", -1, 0),
+    ("d_transpose", -1, 0),
     ("exponent", 0, 0),
-    ("finish", -8, None),
+    ("finish", -5, None),
     ("d_gain", -2, 1),
     ("exponent", 0, 1),
     ("grad", 1, 0),
+    ("decode", -3, None),
+    ("gap_sum", -3, None),
+    ("gap_sum", -4, None),
     ("gap", -1, 1),
     ("total_a", 0, None),
     ("total_b", 0, None),
     ("square", -4, None),
-    ("finish", -5, None),
+    ("finish", -6, None),
     ("recip_total", 0, None),
     ("row_min", 1, 0),
     ("grad", 1, 1),
     ("normalise", 0, 0),
-    ("d_transpose", -1, 0),
-    ("d_transpose", -1, 1),
-    ("curvature", -2, None),
-    ("normalise", 0, 1),
-    ("r_quant", 1, None),
-    ("row_min", 1, 1),
-    ("subtract", 0, 0),
-    ("d_gain", -1, 0),
-    ("exponent", 1, 0),
-    ("recip_curv", -2, None),
-    ("d_gain", -1, 1),
-    ("subtract", 0, 1),
     ("r_transpose", 2, None),
+    ("d_gain", -1, 0),
+    ("normalise", 0, 1),
+    ("subtract", 0, 0),
+    ("row_min", 1, 1),
+    ("d_transpose", -1, 1),
+    ("curvature", -4, None),
+    ("square", -3, None),
+    ("recip_curv", -4, None),
+    ("r_gain", 2, None),
+    ("exponent", 1, 0),
+    ("subtract", 0, 1),
+    ("d_gain", -1, 1),
+    ("d_transpose", 0, 0),
     ("exponent", 1, 1),
-    ("gap_sum", -1, None),
     ("gap", 0, 0),
     ("total_a", 1, None),
-    ("ratio_a", -2, None),
-    ("ratio_b", -2, None),
+    ("ratio", -4, None),
+    ("curvature", -3, None),
     ("total_b", 1, None),
-    ("clip", -2, None),
-    ("step", -2, None),
+    ("clip", -4, None),
+    ("recip_curv", -3, None),
+    ("step", -4, None),
     ("recip_total", 1, None),
-    ("r_gain", 2, None),
+    ("r_quant", 2, None),
     ("grad", 2, 0),
+    ("ratio", -3, None),
     ("normalise", 1, 0),
-    ("d_transpose", 0, 0),
     ("d_quant", -1, None),
-    ("scale_step", -3, None),
+    ("d_transpose", 0, 1),
+    ("scale_step", -4, None),
     ("gap", 0, 1),
     ("subtract", 1, 0),
     ("normalise", 1, 1),
-    ("decode", -1, None),
 ]
-FILL = {("gap", -1, 0): 0, ("gap", -1, 1): 1, ("d_gain", -1, 0): 2, ("d_gain", -1, 1): 3}
 
 
 def tile_smoothedfrankwolfesimplexcoding_t_kernel(tc, r, z, p, enc_bytes, enc_scale, g, dec, out):
@@ -106,10 +110,16 @@ def tile_smoothedfrankwolfesimplexcoding_t_kernel(tc, r, z, p, enc_bytes, enc_sc
         enc_s = keep.tile([P, 4], F32, name="enc_s")
         p_sb = keep.tile([P, 4], BF16, name="p_sb")
         g_sb = keep.tile([P, 2, 4], BF16, name="g_sb")
-        enc_wide = keep.tile([P, 4, CODES], BF16, name="enc_wide", align_bytes=64)
-        enc_grp = keep.tile([P, 2, 4, P, 4], BF16, name="enc_grp", align_bytes=64)
-        enc_codes = keep.tile([P, CODES], U32, name="enc_codes", align_bytes=64)
-        enc_scales = keep.tile([P, CODES], U8, name="enc_scales", align_bytes=64)
+        enc_wide, enc_grp, enc_codes, enc_scales = [], [], [], []
+        for q in range(2):
+            t = keep.tile([P, 4, HALF], BF16, name=f"enc_wide{q}", align_bytes=64)
+            enc_wide.append(t)
+            t = keep.tile([P, 4, P, 4], BF16, name=f"enc_grp{q}", align_bytes=64)
+            enc_grp.append(t)
+            t = keep.tile([P, HALF], U32, name=f"enc_codes{q}", align_bytes=64)
+            enc_codes.append(t)
+            t = keep.tile([P, HALF], U8, name=f"enc_scales{q}", align_bytes=64)
+            enc_scales.append(t)
         dec_raw = keep.tile([P, 2, 4, FEATS], BF16, name="dec_raw", align_bytes=64)
         dec_grp = keep.tile([P, 2, FEATS, 4], BF16, name="dec_grp", align_bytes=64)
         dec_codes = keep.tile([P, 2, FEATS], U32, name="dec_codes", align_bytes=64)
@@ -140,7 +150,7 @@ def tile_smoothedfrankwolfesimplexcoding_t_kernel(tc, r, z, p, enc_bytes, enc_sc
             t = pool.tile([P, 2 * P * 4], BF16, name="rp_b", tag="rp_b", bufs=2, align_bytes=64)
             nc.vector.tensor_tensor(
                 out=t[:].rearrange("p (w u e) -> p w u e", u=2, e=2),
-                in0=st.pop(("rt", j))[:].bitcast(BF16).rearrange("p u (w e) -> p w u e", e=2),
+                in0=st["rt", j][:].bitcast(BF16).rearrange("p u (w e) -> p w u e", e=2),
                 in1=p_sb[:].unsqueeze(1).broadcast_to([P, 2 * P, 4]).rearrange("p w (u e) -> p w u e", e=2),
                 op=ALU.mult,
             )
@@ -149,17 +159,16 @@ def tile_smoothedfrankwolfesimplexcoding_t_kernel(tc, r, z, p, enc_bytes, enc_sc
         def r_quant(j):
             c = pool.tile([P, 2 * P], U32, name="rp_codes", tag="rp_codes", bufs=4, align_bytes=64)
             s = pool.tile([P, 2 * P], U8, name="rp_scales", tag="rp_scales", bufs=4, align_bytes=64)
-            nc.vector.quantize_mx(out=c[:].bitcast(FP8X4), scales=s[:], in_=st.pop(("rp", j))[:])
+            nc.vector.quantize_mx(out=c[:].bitcast(FP8X4), scales=s[:], in_=st["rp", j][:])
             st["rq", j] = (c, s)
 
         def grad(n, q):
             c, s = st["rq", n // 2]
             cols = slice((n % 2) * P, (n % 2 + 1) * P)
             t = psum.tile([P, HALF], F32, name="grad", tag="grad", bufs=4)
-            h = slice(q * HALF, (q + 1) * HALF)
             nc.tensor.matmul_mx(
                 out=t[:], lhsT=c[:, cols].bitcast(FP8X4), lhsT_scale=s[:, cols],
-                rhs=enc_codes[:, h].bitcast(FP8X4), rhs_scale=enc_scales[:, h], start=True, stop=True,
+                rhs=enc_codes[q][:].bitcast(FP8X4), rhs_scale=enc_scales[q][:], start=True, stop=True,
             )
             st["grad", n, q] = t
 
@@ -174,7 +183,7 @@ def tile_smoothedfrankwolfesimplexcoding_t_kernel(tc, r, z, p, enc_bytes, enc_sc
 
         def exponent(n, q):
             if q == 0:
-                st["s", n] = pool.tile([P, 2, 4, P], F32, name="s_sb", tag="s_sb", bufs=3)
+                st["s", n] = pool.tile([P, 2, 4, P], F32, name="s_sb", tag="s_sb", bufs=4)
                 st["sums", n] = pool.tile([P, 2], F32, name="sums", tag="sums", bufs=4)
             nc.scalar.activation(
                 out=st["s", n][:, q].rearrange("p t c -> p (t c)"), in_=st["grad", n, q][:], func=ACT.Exp,
@@ -193,7 +202,7 @@ def tile_smoothedfrankwolfesimplexcoding_t_kernel(tc, r, z, p, enc_bytes, enc_sc
 
         def recip_total(n):
             c = pool.tile([P, 1], F32, name="coef", tag="coef", bufs=4)
-            nc.vector.reciprocal(out=c[:], in_=st.pop(("tot", n))[:])
+            nc.vector.reciprocal(out=c[:], in_=st["tot", n][:])
             st["coef", n] = c
 
         def normalise(n, q):
@@ -201,18 +210,18 @@ def tile_smoothedfrankwolfesimplexcoding_t_kernel(tc, r, z, p, enc_bytes, enc_sc
             nc.scalar.activation(out=s, in_=s, func=ACT.Copy, scale=st["coef", n][:])
 
         def subtract(n, q):
-            if q == 0:
-                st["d", n] = pool.tile([P, 2, 4, P], F32, name="d_sb", tag="d_sb", bufs=3)
+            if ("d", n) not in st:
+                st["d", n] = pool.tile([P, 2, 4, P], F32, name="d_sb", tag="d_sb", bufs=4)
             zt = st["z", n // GROUP][:, n % GROUP, q * HALF : (q + 1) * HALF].rearrange("p (c t) -> p t c", t=4)
             nc.gpsimd.tensor_tensor(out=st["d", n][:, q], in0=st["s", n][:, q], in1=zt, op=ALU.subtract)
 
         def gap(n, q):
-            if ("gaps", n // 2) not in st:
-                st["gaps", n // 2] = pool.tile([P, 2, 2], F32, name="gaps", tag="gaps", bufs=4)
+            if ("gaps", n) not in st:
+                st["gaps", n] = pool.tile([P, 2], F32, name="gaps", tag="gaps", bufs=8)
             junk = pool.tile([P, HALF], F32, name="v_junk", tag="v_junk", bufs=4)
             nc.vector.scalar_tensor_tensor(
                 out=junk[:], in0=st["grad", n, q][:], scalar=1.0, in1=st["d", n][:, q].rearrange("p t c -> p (t c)"),
-                op0=ALU.mult, op1=ALU.mult, accum_out=st["gaps", n // 2][:, n % 2, q : q + 1],
+                op0=ALU.mult, op1=ALU.mult, accum_out=st["gaps", n][:, q : q + 1],
             )
 
         def d_transpose(n, q):
@@ -225,7 +234,7 @@ def tile_smoothedfrankwolfesimplexcoding_t_kernel(tc, r, z, p, enc_bytes, enc_sc
             if ("dg", n // 2) not in st:
                 st["dg", n // 2] = pool.tile([P, 2, 2, P, 4], BF16, name="dg_b", tag="dg_b", bufs=2, align_bytes=64)
             nc.vector.tensor_tensor(
-                out=st["dg", n // 2][:, n % 2, q], in0=st.pop(("dt", n, q))[:].rearrange("p t w -> p w t"),
+                out=st["dg", n // 2][:, n % 2, q], in0=st["dt", n, q][:].rearrange("p t w -> p w t"),
                 in1=g_sb[:, q, :].unsqueeze(1).broadcast_to([P, P, 4]), op=ALU.mult,
             )
 
@@ -247,71 +256,75 @@ def tile_smoothedfrankwolfesimplexcoding_t_kernel(tc, r, z, p, enc_bytes, enc_sc
             st["e", n] = t
 
         def square(n):
-            if ("esq", n // 2) not in st:
-                st["esq", n // 2] = pool.tile([P, 2], F32, name="esq", tag="esq", bufs=2)
+            a = pool.tile([P, 1], F32, name="esq", tag="esq", bufs=4)
             junk = pool.tile([P, FEATS], BF16, name="s_junk", tag="s_junk", bufs=2)
-            nc.scalar.activation(out=junk[:], in_=st["e", n][:], func=ACT.Square, accum_out=st["esq", n // 2][:, n % 2 : n % 2 + 1])
+            nc.scalar.activation(out=junk[:], in_=st["e", n][:], func=ACT.Square, accum_out=a[:])
+            st["esq", n] = a
 
-        def curvature(j):
-            t = pool.tile([P, 2], F32, name="den", tag="den", bufs=2)
-            nc.scalar.activation(out=t[:], in_=st["esq", j][:], func=ACT.Copy, scale=K1, bias=K2)
-            st["den", j] = t
+        def curvature(n):
+            t = pool.tile([P, 1], F32, name="den", tag="den", bufs=4)
+            nc.scalar.activation(out=t[:], in_=st["esq", n][:], func=ACT.Copy, scale=K1, bias=K2)
+            st["den", n] = t
 
-        def recip_curv(j):
-            t = pool.tile([P, 2], F32, name="rden", tag="rden", bufs=3)
-            nc.vector.reciprocal(out=t[:], in_=st.pop(("den", j))[:])
-            st["rden", j] = t
+        def recip_curv(n):
+            t = pool.tile([P, 1], F32, name="rden", tag="rden", bufs=4)
+            nc.vector.reciprocal(out=t[:], in_=st["den", n][:])
+            st["rden", n] = t
 
-        def gap_sum(j):
-            u = pool.tile([P, 2], F32, name="gsum", tag="gsum", bufs=4)
-            nc.vector.tensor_reduce(out=u[:], in_=st["gaps", j][:], axis=mybir.AxisListType.X, op=ALU.add)
-            st["gsum", j] = u
+        def gap_sum(n):
+            u = pool.tile([P, 1], F32, name="gsum", tag="gsum", bufs=8)
+            nc.vector.tensor_reduce(out=u[:], in_=st["gaps", n][:], axis=mybir.AxisListType.X, op=ALU.add)
+            st["gsum", n] = u
 
-        def ratio(j, i):
-            if ("gam_a", j) not in st:
-                st["gam_a", j] = pool.tile([P, 2], F32, name="gam_a", tag="gam_a", bufs=2)
-            a = st["gam_a", j]
-            nc.scalar.activation(out=a[:, i : i + 1], in_=st["gsum", j][:, i : i + 1], func=ACT.Relu, scale=st["rden", j][:, i : i + 1])
+        def ratio(n):
+            a = pool.tile([P, 1], F32, name="gam_a", tag="gam_a", bufs=4)
+            nc.scalar.activation(out=a[:], in_=st["gsum", n][:], func=ACT.Relu, scale=st["rden", n][:])
+            st["gam_a", n] = a
 
-        def ratio_a(j):
-            ratio(j, 0)
+        def clip(n):
+            b = pool.tile([P, 1], F32, name="gam_b", tag="gam_b", bufs=4)
+            nc.scalar.activation(out=b[:], in_=st["gam_a", n][:], func=ACT.Relu, scale=-1.0, bias=1.0)
+            st["gam_b", n] = b
 
-        def ratio_b(j):
-            ratio(j, 1)
-
-        def clip(j):
-            b = pool.tile([P, 2], F32, name="gam_b", tag="gam_b", bufs=2)
-            nc.scalar.activation(out=b[:], in_=st["gam_a", j][:], func=ACT.Relu, scale=-1.0, bias=1.0)
-            st["gam_b", j] = b
-
-        def step(j):
-            c = pool.tile([P, 2], F32, name="gam_c", tag="gam_c", bufs=3)
-            nc.scalar.activation(out=c[:], in_=st["gam_b", j][:], func=ACT.Copy, scale=-1.0, bias=1.0)
-            st["gam", j] = c
+        def step(n):
+            c = pool.tile([P, 1], F32, name="gam_c", tag="gam_c", bufs=4)
+            nc.scalar.activation(out=c[:], in_=st["gam_b", n][:], func=ACT.Copy, scale=-1.0, bias=1.0)
+            st["gam", n] = c
 
         def scale_step(n):
-            t = pool.tile([P, FEATS], F32, name="ge", tag="ge", bufs=4)
-            nc.scalar.activation(out=t[:], in_=st.pop(("e", n))[:], func=ACT.Copy, scale=st["gam", n // 2][:, n % 2 : n % 2 + 1])
-            st["ge", n] = t
+            rt = st["r", n // GROUP][:, n % GROUP, :]
+            if n < NT - VFIN:
+                t = pool.tile([P, FEATS], F32, name="ge", tag="ge", bufs=4)
+                nc.scalar.activation(out=t[:], in_=st["e", n][:], func=ACT.Copy, scale=st["gam", n][:])
+                st["ge", n] = t
+            else:
+                o = pool.tile([P, FEATS], F32, name="o_sb", tag="o_sb", bufs=4)
+                nc.vector.scalar_tensor_tensor(out=o[:], in0=st["e", n][:], scalar=st["gam", n][:], in1=rt, op0=ALU.mult, op1=ALU.add)
+                nc.sync.dma_start(out=out_hbm[n // GROUP][:, n % GROUP, :], in_=o[:])
 
         def finish(n):
-            t = pool.tile([P, FEATS], F32, name="o_sb", tag="o_sb", bufs=4)
-            nc.gpsimd.tensor_tensor(out=t[:], in0=st.pop(("ge", n))[:], in1=st["r", n // GROUP][:, n % GROUP, :], op=ALU.add)
-            nc.sync.dma_start(out=out_hbm[n // GROUP][:, n % GROUP, :], in_=t[:])
+            if n < NT - VFIN:
+                t = pool.tile([P, FEATS], F32, name="o_sb", tag="o_sb", bufs=4)
+                nc.gpsimd.tensor_tensor(out=t[:], in0=st["ge", n][:], in1=st["r", n // GROUP][:, n % GROUP, :], op=ALU.add)
+                nc.sync.dma_start(out=out_hbm[n // GROUP][:, n % GROUP, :], in_=t[:])
 
         def widen(q):
             h = slice(q * HALF, (q + 1) * HALF)
-            for t in (1, 2, 3):
-                nc.scalar.activation(out=enc_wide[:, t, h], in_=enc_u8[:, t, h].bitcast(FP8), func=ACT.Copy, scale=enc_s[:, t : t + 1])
-            nc.vector.tensor_scalar(out=enc_wide[:, 0, h], in0=enc_u8[:, 0, h].bitcast(FP8), scalar1=enc_s[:, 0:1], scalar2=None, op0=ALU.mult)
+            for t in (2, 3):
+                nc.scalar.activation(out=enc_wide[q][:, t, :], in_=enc_u8[:, t, h].bitcast(FP8), func=ACT.Copy, scale=enc_s[:, t : t + 1])
+            for t in (0, 1):
+                nc.vector.tensor_scalar(out=enc_wide[q][:, t, :], in0=enc_u8[:, t, h].bitcast(FP8), scalar1=enc_s[:, t : t + 1], scalar2=None, op0=ALU.mult)
 
         def enc_interleave(q):
-            h = slice(q * HALF, (q + 1) * HALF)
-            nc.vector.tensor_copy(out=enc_grp[:, q], in_=enc_wide[:, :, h].rearrange("p t (c u) -> p u c t", u=4))
+            src = enc_wide[q][:].rearrange("p t (c u) -> p u c t", u=4)
+            if q == 0:
+                nc.vector.tensor_copy(out=enc_grp[q][:], in_=src)
+            else:
+                for v in (0, 2):
+                    nc.scalar.copy(out=enc_grp[q][:, v : v + 2], in_=src[:, v : v + 2])
 
         def enc_quant(q):
-            h = slice(q * HALF, (q + 1) * HALF)
-            nc.vector.quantize_mx(out=enc_codes[:, h].bitcast(FP8X4), scales=enc_scales[:, h], in_=enc_grp[:, q].rearrange("p u c t -> p (u c t)"))
+            nc.vector.quantize_mx(out=enc_codes[q][:].bitcast(FP8X4), scales=enc_scales[q][:], in_=enc_grp[q][:].rearrange("p u c t -> p (u c t)"))
 
         def dec_piece(i):
             q, m = i // 2, slice((i % 2) * 256, (i % 2 + 1) * 256)
@@ -329,6 +342,7 @@ def tile_smoothedfrankwolfesimplexcoding_t_kernel(tc, r, z, p, enc_bytes, enc_sc
         nc.sync.dma_start(out=dec_raw[:], in_=dec.rearrange("(q p t) m -> p q t m", p=P, t=4))
         load_r(1)
         load_z(1)
+        load_r(2)
         nc.vector.memset(warm[:], 0.0)
         nc.scalar.activation(out=warm[:, 1:2], in_=warm[:, 0:1], func=ACT.Exp)
         make_identity(nc, ident[:])
@@ -337,39 +351,51 @@ def tile_smoothedfrankwolfesimplexcoding_t_kernel(tc, r, z, p, enc_bytes, enc_sc
             "r_transpose": r_transpose, "r_gain": r_gain, "r_quant": r_quant, "grad": grad, "row_min": row_min, "exponent": exponent,
             "total_a": total_a, "total_b": total_b, "recip_total": recip_total, "normalise": normalise, "subtract": subtract, "gap": gap,
             "d_transpose": d_transpose, "d_gain": d_gain, "d_quant": d_quant, "decode": decode, "square": square, "curvature": curvature,
-            "recip_curv": recip_curv, "gap_sum": gap_sum, "ratio_a": ratio_a, "ratio_b": ratio_b, "clip": clip, "step": step,
+            "recip_curv": recip_curv, "gap_sum": gap_sum, "ratio": ratio, "clip": clip, "step": step,
             "scale_step": scale_step, "finish": finish,
         }
-        by_pair = {"r_transpose", "r_gain", "r_quant", "d_quant", "curvature", "recip_curv", "gap_sum", "ratio_a", "ratio_b", "clip", "step"}
+        by_pair = {"r_transpose", "r_gain", "r_quant", "d_quant"}
 
         def period(k):
-            if k > 0 and k % 2 == 0 and k // 2 + 1 < NGROUP:
-                load_r(k // 2 + 1)
-                load_z(k // 2 + 1)
+            if k > 0 and k % 2 == 0:
+                if k // 2 + 2 < NGROUP:
+                    load_r(k // 2 + 2)
+                if k // 2 + 1 < NGROUP:
+                    load_z(k // 2 + 1)
             for name, off, q in PLAN:
                 if name in by_pair:
                     if 0 <= k + off < NPAIR:
                         stages[name](k + off)
-                    elif name == "d_quant" and k + off == -1:
-                        dec_quant(0)
-                        dec_quant(1)
+                    n = k + off
                 else:
                     n = 2 * k + off
-                    if (name, n, q) in FILL:
-                        dec_piece(FILL[name, n, q])
                     if 0 <= n < NT:
                         if q is None:
                             stages[name](n)
                         else:
                             stages[name](n, q)
+                for task in FILL.get((name, n, q), ()):
+                    task()
 
+        FILL = {
+            ("gap", -1, 0): [lambda: dec_piece(0)],
+            ("gap", -1, 1): [lambda: dec_piece(1)],
+            ("d_gain", -1, 0): [lambda: dec_piece(2)],
+            ("d_gain", -1, 1): [lambda: dec_piece(3)],
+            ("d_quant", -1, None): [lambda: dec_quant(0), lambda: dec_quant(1)],
+        }
         widen(0)
         widen(1)
-        period(-2)
+        r_transpose(0)
+        r_transpose(1)
         enc_interleave(0)
-        enc_quant(0)
-        period(-1)
         enc_interleave(1)
+        r_gain(0)
+        enc_quant(0)
+        r_quant(0)
+        grad(0, 0)
+        r_gain(1)
         enc_quant(1)
-        for k in range(NPAIR + 5):
+        r_quant(1)
+        for k in range(NPAIR + 6):
             period(k)

@@ -18,384 +18,373 @@ ALU = mybir.AluOpType
 ACT = mybir.ActivationFunctionType
 
 P = 128
-GROUP = 4
-NT = ROWS // P
-NPAIR = NT // 2
-NGROUP = NT // GROUP
+PACK = 4
 HALF = 512
-K1 = -math.sqrt(FEATS * CODES) / FEATS
-K2 = -math.sqrt(FEATS * CODES) * 1e-6
-VFIN = 4
-PLAN = [
-    ("row_min", 0, 0),
-    ("grad", 0, 1),
-    ("clip", -5, None),
-    ("step", -5, None),
-    ("d_gain", -2, 0),
-    ("scale_step", -5, None),
-    ("decode", -4, None),
-    ("subtract", -1, 1),
-    ("row_min", 0, 1),
-    ("gap", -1, 0),
-    ("d_transpose", -1, 0),
-    ("exponent", 0, 0),
-    ("finish", -5, None),
-    ("d_gain", -2, 1),
-    ("exponent", 0, 1),
-    ("grad", 1, 0),
-    ("decode", -3, None),
-    ("gap_sum", -3, None),
-    ("gap_sum", -4, None),
-    ("gap", -1, 1),
-    ("total_a", 0, None),
-    ("total_b", 0, None),
-    ("square", -4, None),
-    ("finish", -6, None),
-    ("recip_total", 0, None),
-    ("row_min", 1, 0),
-    ("grad", 1, 1),
-    ("normalise", 0, 0),
-    ("r_transpose", 2, None),
-    ("d_gain", -1, 0),
-    ("normalise", 0, 1),
-    ("subtract", 0, 0),
-    ("row_min", 1, 1),
-    ("d_transpose", -1, 1),
-    ("curvature", -4, None),
-    ("square", -3, None),
-    ("recip_curv", -4, None),
-    ("r_gain", 2, None),
-    ("exponent", 1, 0),
-    ("subtract", 0, 1),
-    ("d_gain", -1, 1),
-    ("d_transpose", 0, 0),
-    ("exponent", 1, 1),
-    ("gap", 0, 0),
-    ("total_a", 1, None),
-    ("ratio", -4, None),
-    ("curvature", -3, None),
-    ("total_b", 1, None),
-    ("clip", -4, None),
-    ("recip_curv", -3, None),
-    ("step", -4, None),
-    ("recip_total", 1, None),
-    ("r_quant", 2, None),
-    ("grad", 2, 0),
-    ("ratio", -3, None),
-    ("normalise", 1, 0),
-    ("d_quant", -1, None),
-    ("d_transpose", 0, 1),
-    ("scale_step", -4, None),
-    ("gap", 0, 1),
-    ("subtract", 1, 0),
-    ("normalise", 1, 1),
-]
+GROUP = 4
+TILES = ROWS // P
+PAIRS = TILES // 2
+GROUPS = TILES // GROUP
+VECTOR_TAIL = 6
+STATS = 8
+
+GAP_SCALE = -math.sqrt(FEATS * CODES)
 
 
 def tile_smoothedfrankwolfesimplexcoding_t_kernel(tc, r, z, p, enc_bytes, enc_scale, g, dec, out):
     nc = tc.nc
-    r_hbm = r.rearrange("(g p j) m -> g p j m", p=P, j=GROUP)
-    z_hbm = z.rearrange("(g p j) k -> g p j k", p=P, j=GROUP)
-    out_hbm = out.rearrange("(g p j) m -> g p j m", p=P, j=GROUP)
+    r_hbm = r.rearrange("(m w j) f -> m w j f", w=P, j=GROUP)
+    z_hbm = z.rearrange("(m w j) k -> m w j k", w=P, j=GROUP)
+    out_hbm = out.rearrange("(m w j) f -> m w j f", w=P, j=GROUP)
 
     with ExitStack() as ctx:
         keep = ctx.enter_context(tc.tile_pool(name="keep", bufs=1))
-        pool = ctx.enter_context(tc.tile_pool(name="work", bufs=2))
+        work = ctx.enter_context(tc.tile_pool(name="work", bufs=2))
         psum = ctx.enter_context(tc.psum_pool(name="psum", bufs=2))
         ctx.enter_context(tc.manual_schedule())
 
-        ident = keep.tile([P, P], F32, name="ident")
-        warm = keep.tile([P, 2], F32, name="warm")
-        enc_u8 = keep.tile([P, 4, CODES], U8, name="enc_u8", align_bytes=64)
-        enc_s = keep.tile([P, 4], F32, name="enc_s")
-        p_sb = keep.tile([P, 4], BF16, name="p_sb")
-        g_sb = keep.tile([P, 2, 4], BF16, name="g_sb")
-        enc_wide, enc_grp, enc_codes, enc_scales = [], [], [], []
+        identity = keep.tile([P, P], F32, name="identity")
+        table = keep.tile([P, 2], F32, name="table")
+        p_sb = keep.tile([P, PACK], BF16, name="p_sb")
+        g_sb = keep.tile([P, 2, PACK], BF16, name="g_sb")
+        enc_u8 = keep.tile([P, PACK, CODES], U8, name="enc_u8", align_bytes=64)
+        enc_s = keep.tile([P, PACK], F32, name="enc_s")
+        dec_raw = keep.tile([P, 2, PACK, FEATS], BF16, name="dec_raw", align_bytes=64)
+        enc_wide, enc_words, enc_codes, enc_scales, dec_words, dec_codes, dec_scales = [], [], [], [], [], [], []
         for q in range(2):
-            t = keep.tile([P, 4, HALF], BF16, name=f"enc_wide{q}", align_bytes=64)
-            enc_wide.append(t)
-            t = keep.tile([P, 4, P, 4], BF16, name=f"enc_grp{q}", align_bytes=64)
-            enc_grp.append(t)
-            t = keep.tile([P, HALF], U32, name=f"enc_codes{q}", align_bytes=64)
-            enc_codes.append(t)
-            t = keep.tile([P, HALF], U8, name=f"enc_scales{q}", align_bytes=64)
-            enc_scales.append(t)
-        dec_raw = keep.tile([P, 2, 4, FEATS], BF16, name="dec_raw", align_bytes=64)
-        dec_grp = keep.tile([P, 2, FEATS, 4], BF16, name="dec_grp", align_bytes=64)
-        dec_codes = keep.tile([P, 2, FEATS], U32, name="dec_codes", align_bytes=64)
-        dec_scales = keep.tile([P, 2, FEATS], U8, name="dec_scales", align_bytes=64)
+            wide = keep.tile([P, PACK, HALF], BF16, name=f"enc_wide{q}", align_bytes=64)
+            words = keep.tile([P, PACK, P, PACK], BF16, name=f"enc_words{q}", align_bytes=64)
+            codes = keep.tile([P, HALF], U32, name=f"enc_codes{q}", align_bytes=64)
+            scales = keep.tile([P, HALF], U8, name=f"enc_scales{q}", align_bytes=64)
+            enc_wide.append(wide)
+            enc_words.append(words)
+            enc_codes.append(codes)
+            enc_scales.append(scales)
+            words = keep.tile([P, FEATS, PACK], BF16, name=f"dec_words{q}", align_bytes=64)
+            codes = keep.tile([P, FEATS], U32, name=f"dec_codes{q}", align_bytes=64)
+            scales = keep.tile([P, FEATS], U8, name=f"dec_scales{q}", align_bytes=64)
+            dec_words.append(words)
+            dec_codes.append(codes)
+            dec_scales.append(scales)
 
-        st = {}
+        live = {}
 
-        def load_r(k):
-            t = pool.tile([P, GROUP, FEATS], BF16, name="r_sb", tag="r_sb", bufs=6, align_bytes=64)
-            nc.sync.dma_start(out=t[:], in_=r_hbm[k])
-            st["r", k] = t
+        def column(name):
+            return work.tile([P, 1], F32, name=name, tag=name, bufs=STATS)
 
-        def load_z(k):
-            t = pool.tile([P, GROUP, CODES], BF16, name="z_sb", tag="z_sb", bufs=3, align_bytes=64)
-            nc.sync.dma_start(out=t[:], in_=z_hbm[k])
-            st["z", k] = t
+
+        def load_r(m, parts=1):
+            tile = work.tile([P, GROUP, FEATS], BF16, name="r_sb", tag="r_sb", bufs=6, align_bytes=64)
+            width = GROUP // parts
+            for j in range(0, GROUP, width):
+                nc.sync.dma_start(out=tile[:, j : j + width], in_=r_hbm[m][:, j : j + width])
+            live["r", m] = tile
+
+        def load_z(m):
+            tile = work.tile([P, GROUP, CODES], BF16, name="z_sb", tag="z_sb", bufs=3, align_bytes=64)
+            nc.sync.dma_start(out=tile[:], in_=z_hbm[m])
+            live["z", m] = tile
+
+        def rows_of(name, n):
+            return live[name, n // GROUP][:, n % GROUP, :]
+
+
+        def enc_widen(q):
+            for t in range(PACK):
+                plane = enc_u8[:, t, q * HALF : (q + 1) * HALF].bitcast(FP8)
+                if t >= (3 if q == 0 else 2):
+                    nc.scalar.activation(out=enc_wide[q][:, t, :], in_=plane, func=ACT.Copy, scale=enc_s[:, t : t + 1])
+                else:
+                    nc.vector.tensor_scalar(
+                        out=enc_wide[q][:, t, :], in0=plane, scalar1=enc_s[:, t : t + 1], scalar2=None, op0=ALU.mult
+                    )
+
+        def enc_interleave(q):
+            source = enc_wide[q][:].rearrange("w t (c u) -> w u c t", u=PACK)
+            if q == 0:
+                nc.vector.tensor_copy(out=enc_words[q][:], in_=source)
+            else:
+                for u in (0, 2):
+                    nc.scalar.copy(out=enc_words[q][:, u : u + 2], in_=source[:, u : u + 2])
+
+        def enc_quantise(q):
+            nc.vector.quantize_mx(
+                out=enc_codes[q][:].bitcast(FP8X4), scales=enc_scales[q][:],
+                in_=enc_words[q][:].rearrange("w u c t -> w (u c t)"),
+            )
+
+        def dec_interleave(q, part):
+            f = slice(part * FEATS // 2, (part + 1) * FEATS // 2)
+            source = dec_raw[:, q, :, f].rearrange("w t f -> w f t")
+            if q == 0:
+                nc.scalar.copy(out=dec_words[q][:, f, :], in_=source)
+            else:
+                nc.vector.tensor_copy(out=dec_words[q][:, f, :], in_=source)
+
+        def dec_quantise(q):
+            nc.vector.quantize_mx(
+                out=dec_codes[q][:].bitcast(FP8X4), scales=dec_scales[q][:],
+                in_=dec_words[q][:].rearrange("w f t -> w (f t)"),
+            )
+
 
         def r_transpose(j):
-            t = psum.tile([P, 2, 2 * P], F32, name="t_ps", tag="t_ps", bufs=2)
+            bank = psum.tile([P, 2, 2 * P], F32, name="turned", tag="turned", bufs=2)
             for i in range(2):
-                n = 2 * j + i
-                words = st["r", n // GROUP][:, n % GROUP, :].bitcast(F32)
+                words = rows_of("r", 2 * j + i).bitcast(F32)
                 for u in range(2):
-                    nc.tensor.transpose(t[:, u, i * P : (i + 1) * P], words[:, u : 2 * P : 2], ident[:])
-            st["rt", j] = t
+                    nc.tensor.transpose(bank[:, u, i * P : (i + 1) * P], words[:, u : 2 * P : 2], identity[:])
+            live["r_turned", j] = bank
 
         def r_gain(j):
-            t = pool.tile([P, 2 * P * 4], BF16, name="rp_b", tag="rp_b", bufs=2, align_bytes=64)
+            tile = work.tile([P, 2 * P * PACK], BF16, name="rp", tag="rp", bufs=2, align_bytes=64)
             nc.vector.tensor_tensor(
-                out=t[:].rearrange("p (w u e) -> p w u e", u=2, e=2),
-                in0=st["rt", j][:].bitcast(BF16).rearrange("p u (w e) -> p w u e", e=2),
-                in1=p_sb[:].unsqueeze(1).broadcast_to([P, 2 * P, 4]).rearrange("p w (u e) -> p w u e", e=2),
+                out=tile[:].rearrange("w (n u e) -> w n u e", u=2, e=2),
+                in0=live["r_turned", j][:].bitcast(BF16).rearrange("w u (n e) -> w n u e", e=2),
+                in1=p_sb[:].unsqueeze(1).broadcast_to([P, 2 * P, PACK]).rearrange("w n (u e) -> w n u e", e=2),
                 op=ALU.mult,
             )
-            st["rp", j] = t
+            live["rp", j] = tile
 
-        def r_quant(j):
-            c = pool.tile([P, 2 * P], U32, name="rp_codes", tag="rp_codes", bufs=4, align_bytes=64)
-            s = pool.tile([P, 2 * P], U8, name="rp_scales", tag="rp_scales", bufs=4, align_bytes=64)
-            nc.vector.quantize_mx(out=c[:].bitcast(FP8X4), scales=s[:], in_=st["rp", j][:])
-            st["rq", j] = (c, s)
+        def r_quantise(j):
+            codes = work.tile([P, 2 * P], U32, name="rp_codes", tag="rp_codes", bufs=4, align_bytes=64)
+            scales = work.tile([P, 2 * P], U8, name="rp_scales", tag="rp_scales", bufs=4, align_bytes=64)
+            nc.vector.quantize_mx(out=codes[:].bitcast(FP8X4), scales=scales[:], in_=live["rp", j][:])
+            live["rp_mx", j] = codes, scales
+
 
         def grad(n, q):
-            c, s = st["rq", n // 2]
-            cols = slice((n % 2) * P, (n % 2 + 1) * P)
-            t = psum.tile([P, HALF], F32, name="grad", tag="grad", bufs=4)
+            codes, scales = live["rp_mx", n // 2]
+            rows = slice(n % 2 * P, (n % 2 + 1) * P)
+            bank = psum.tile([P, HALF], F32, name="grad", tag="grad", bufs=4)
             nc.tensor.matmul_mx(
-                out=t[:], lhsT=c[:, cols].bitcast(FP8X4), lhsT_scale=s[:, cols],
+                out=bank[:], lhsT=codes[:, rows].bitcast(FP8X4), lhsT_scale=scales[:, rows],
                 rhs=enc_codes[q][:].bitcast(FP8X4), rhs_scale=enc_scales[q][:], start=True, stop=True,
             )
-            st["grad", n, q] = t
+            live["grad", n, q] = bank
 
         def row_min(n, q):
-            junk = pool.tile([P, HALF], F32, name="v_junk", tag="v_junk", bufs=4)
-            m = pool.tile([P, 1], F32, name="row_min", tag="row_min", bufs=6)
+            unused = work.tile([P, HALF], F32, name="unused", tag="unused", bufs=4)
+            least = column("least")
             nc.vector.tensor_scalar(
-                out=junk[:], in0=st["grad", n, q][:], scalar1=2.0, scalar2=None if q == 0 else st["min", n][:],
-                op0=ALU.mult, op1=ALU.min, accum_out=m[:],
+                out=unused[:], in0=live["grad", n, q][:], scalar1=2.0, scalar2=None if q == 0 else live["least", n][:],
+                op0=ALU.mult, op1=ALU.min, accum_out=least[:],
             )
-            st["min", n] = m
+            live["least", n] = least
 
         def exponent(n, q):
             if q == 0:
-                st["s", n] = pool.tile([P, 2, 4, P], F32, name="s_sb", tag="s_sb", bufs=4)
-                st["sums", n] = pool.tile([P, 2], F32, name="sums", tag="sums", bufs=4)
+                live["s", n] = work.tile([P, 2, PACK, P], F32, name="s_sb", tag="s_sb", bufs=4)
+                live["sums", n] = work.tile([P, 2], F32, name="sums", tag="sums", bufs=STATS)
             nc.scalar.activation(
-                out=st["s", n][:, q].rearrange("p t c -> p (t c)"), in_=st["grad", n, q][:], func=ACT.Exp,
-                scale=-2.0, bias=st["min", n][:], accum_out=st["sums", n][:, q : q + 1],
+                out=live["s", n][:, q].rearrange("n u c -> n (u c)"), in_=live["grad", n, q][:], func=ACT.Exp,
+                scale=-2.0, bias=live["least", n][:], accum_out=live["sums", n][:, q : q + 1],
             )
 
         def total_a(n):
-            a = pool.tile([P, 1], F32, name="sum_a", tag="sum_a", bufs=4)
-            nc.scalar.activation(out=a[:], in_=st["sums", n][:, 0:1], func=ACT.Copy, scale=1.0 / RADIUS)
-            st["sum_a", n] = a
+            live["sum_a", n] = column("sum_a")
+            nc.scalar.activation(out=live["sum_a", n][:], in_=live["sums", n][:, 0:1], func=ACT.Copy, scale=1.0 / RADIUS)
 
         def total_b(n):
-            b = pool.tile([P, 1], F32, name="sum_b", tag="sum_b", bufs=4)
-            nc.scalar.activation(out=b[:], in_=st["sums", n][:, 1:2], func=ACT.Identity, scale=1.0 / RADIUS, bias=st["sum_a", n][:])
-            st["tot", n] = b
+            live["sum_b", n] = column("sum_b")
+            nc.scalar.activation(
+                out=live["sum_b", n][:], in_=live["sums", n][:, 1:2], func=ACT.Identity,
+                scale=1.0 / RADIUS, bias=live["sum_a", n][:],
+            )
 
         def recip_total(n):
-            c = pool.tile([P, 1], F32, name="coef", tag="coef", bufs=4)
-            nc.vector.reciprocal(out=c[:], in_=st["tot", n][:])
-            st["coef", n] = c
+            live["coef", n] = column("coef")
+            nc.vector.reciprocal(out=live["coef", n][:], in_=live["sum_b", n][:])
 
         def normalise(n, q):
-            s = st["s", n][:, q].rearrange("p t c -> p (t c)")
-            nc.scalar.activation(out=s, in_=s, func=ACT.Copy, scale=st["coef", n][:])
+            half = live["s", n][:, q].rearrange("n u c -> n (u c)")
+            nc.scalar.activation(out=half, in_=half, func=ACT.Copy, scale=live["coef", n][:])
 
         def subtract(n, q):
-            if ("d", n) not in st:
-                st["d", n] = pool.tile([P, 2, 4, P], F32, name="d_sb", tag="d_sb", bufs=4)
-            zt = st["z", n // GROUP][:, n % GROUP, q * HALF : (q + 1) * HALF].rearrange("p (c t) -> p t c", t=4)
-            nc.gpsimd.tensor_tensor(out=st["d", n][:, q], in0=st["s", n][:, q], in1=zt, op=ALU.subtract)
+            if q == 0:
+                live["d", n] = work.tile([P, 2, PACK, P], F32, name="d_sb", tag="d_sb", bufs=4)
+            z_half = rows_of("z", n)[:, q * HALF : (q + 1) * HALF].rearrange("n (c u) -> n u c", u=PACK)
+            nc.gpsimd.tensor_tensor(out=live["d", n][:, q], in0=live["s", n][:, q], in1=z_half, op=ALU.subtract)
 
         def gap(n, q):
-            if ("gaps", n) not in st:
-                st["gaps", n] = pool.tile([P, 2], F32, name="gaps", tag="gaps", bufs=8)
-            junk = pool.tile([P, HALF], F32, name="v_junk", tag="v_junk", bufs=4)
+            if q == 0:
+                live["gaps", n] = work.tile([P, 2], F32, name="gaps", tag="gaps", bufs=STATS)
+            unused = work.tile([P, HALF], F32, name="unused", tag="unused", bufs=4)
             nc.vector.scalar_tensor_tensor(
-                out=junk[:], in0=st["grad", n, q][:], scalar=1.0, in1=st["d", n][:, q].rearrange("p t c -> p (t c)"),
-                op0=ALU.mult, op1=ALU.mult, accum_out=st["gaps", n][:, q : q + 1],
+                out=unused[:], in0=live["grad", n, q][:], scalar=1.0, in1=live["d", n][:, q].rearrange("n u c -> n (u c)"),
+                op0=ALU.mult, op1=ALU.mult, accum_out=live["gaps", n][:, q : q + 1],
             )
-
-        def d_transpose(n, q):
-            t = psum.tile([P, 4, P], F32, name="t_ps", tag="t_ps", bufs=2)
-            for i in range(4):
-                nc.tensor.transpose(t[:, i, :], st["d", n][:, q, i, :], ident[:])
-            st["dt", n, q] = t
-
-        def d_gain(n, q):
-            if ("dg", n // 2) not in st:
-                st["dg", n // 2] = pool.tile([P, 2, 2, P, 4], BF16, name="dg_b", tag="dg_b", bufs=2, align_bytes=64)
-            nc.vector.tensor_tensor(
-                out=st["dg", n // 2][:, n % 2, q], in0=st["dt", n, q][:].rearrange("p t w -> p w t"),
-                in1=g_sb[:, q, :].unsqueeze(1).broadcast_to([P, P, 4]), op=ALU.mult,
-            )
-
-        def d_quant(j):
-            c = pool.tile([P, 4 * P], U32, name="d_codes", tag="d_codes", bufs=2, align_bytes=64)
-            s = pool.tile([P, 4 * P], U8, name="d_scales", tag="d_scales", bufs=2, align_bytes=64)
-            nc.vector.quantize_mx(out=c[:].bitcast(FP8X4), scales=s[:], in_=st["dg", j][:].rearrange("p i q w t -> p (i q w t)"))
-            st["dq", j] = (c, s)
-
-        def decode(n):
-            c, s = st["dq", n // 2]
-            t = psum.tile([P, FEATS], F32, name="e_ps", tag="e_ps", bufs=2)
-            for q in range(2):
-                cols = slice(((n % 2) * 2 + q) * P, ((n % 2) * 2 + q + 1) * P)
-                nc.tensor.matmul_mx(
-                    out=t[:], lhsT=c[:, cols].bitcast(FP8X4), lhsT_scale=s[:, cols],
-                    rhs=dec_codes[:, q, :].bitcast(FP8X4), rhs_scale=dec_scales[:, q, :], start=(q == 0), stop=(q == 1),
-                )
-            st["e", n] = t
-
-        def square(n):
-            a = pool.tile([P, 1], F32, name="esq", tag="esq", bufs=4)
-            junk = pool.tile([P, FEATS], BF16, name="s_junk", tag="s_junk", bufs=2)
-            nc.scalar.activation(out=junk[:], in_=st["e", n][:], func=ACT.Square, accum_out=a[:])
-            st["esq", n] = a
-
-        def curvature(n):
-            t = pool.tile([P, 1], F32, name="den", tag="den", bufs=4)
-            nc.scalar.activation(out=t[:], in_=st["esq", n][:], func=ACT.Copy, scale=K1, bias=K2)
-            st["den", n] = t
-
-        def recip_curv(n):
-            t = pool.tile([P, 1], F32, name="rden", tag="rden", bufs=4)
-            nc.vector.reciprocal(out=t[:], in_=st["den", n][:])
-            st["rden", n] = t
 
         def gap_sum(n):
-            u = pool.tile([P, 1], F32, name="gsum", tag="gsum", bufs=8)
-            nc.vector.tensor_reduce(out=u[:], in_=st["gaps", n][:], axis=mybir.AxisListType.X, op=ALU.add)
-            st["gsum", n] = u
+            live["gap", n] = column("gap")
+            nc.vector.tensor_reduce(out=live["gap", n][:], in_=live["gaps", n][:], axis=mybir.AxisListType.X, op=ALU.add)
+
+
+        def d_transpose(n, q):
+            bank = psum.tile([P, PACK, P], F32, name="turned", tag="turned", bufs=2)
+            for u in range(PACK):
+                nc.tensor.transpose(bank[:, u, :], live["d", n][:, q, u, :], identity[:])
+            live["d_turned", n, q] = bank
+
+        def d_gain(n, q):
+            if ("dg", n // 2) not in live:
+                live["dg", n // 2] = work.tile([P, 2, 2, P, PACK], BF16, name="dg", tag="dg", bufs=2, align_bytes=64)
+            nc.vector.tensor_tensor(
+                out=live["dg", n // 2][:, n % 2, q], in0=live["d_turned", n, q][:].rearrange("w t n -> w n t"),
+                in1=g_sb[:, q, :].unsqueeze(1).broadcast_to([P, P, PACK]), op=ALU.mult,
+            )
+            if n == TILES - 2 and q == 1:
+                quantise_tiles(n, 1)
+
+        def quantise_tiles(n, count):
+            j = n // 2
+            if ("dg_mx", j) not in live:
+                codes = work.tile([P, 2, 2 * P], U32, name="dg_codes", tag="dg_codes", bufs=2, align_bytes=64)
+                scales = work.tile([P, 2, 2 * P], U8, name="dg_scales", tag="dg_scales", bufs=2, align_bytes=64)
+                live["dg_mx", j] = codes, scales
+            codes, scales = live["dg_mx", j]
+            i = slice(n % 2, n % 2 + count)
+            nc.vector.quantize_mx(
+                out=codes[:, i].rearrange("w i n -> w (i n)").bitcast(FP8X4), scales=scales[:, i].rearrange("w i n -> w (i n)"),
+                in_=live["dg", j][:, i].rearrange("w i q n t -> w (i q n t)"),
+            )
+
+        def d_quantise(j):
+            if j < PAIRS - 1:
+                quantise_tiles(2 * j, 2)
+            else:
+                quantise_tiles(2 * j + 1, 1)
+
+        def decode(n):
+            codes, scales = live["dg_mx", n // 2]
+            tag, bufs = ("decoded", 2) if n < TILES - 2 else ("grad", 4)
+            bank = psum.tile([P, FEATS], F32, name="decoded", tag=tag, bufs=bufs)
+            for q in range(2):
+                rows = slice(q * P, (q + 1) * P)
+                nc.tensor.matmul_mx(
+                    out=bank[:], lhsT=codes[:, n % 2, rows].bitcast(FP8X4), lhsT_scale=scales[:, n % 2, rows],
+                    rhs=dec_codes[q][:].bitcast(FP8X4), rhs_scale=dec_scales[q][:], start=(q == 0), stop=(q == 1),
+                )
+            live["e", n] = bank
+
+
+        def square(n):
+            unused = work.tile([P, FEATS], BF16, name="squares", tag="squares", bufs=2)
+            live["e_sq", n] = column("e_sq")
+            nc.scalar.activation(out=unused[:], in_=live["e", n][:], func=ACT.Square, accum_out=live["e_sq", n][:])
+
+        def curvature(n):
+            live["curv", n] = column("curv")
+            nc.scalar.activation(
+                out=live["curv", n][:], in_=live["e_sq", n][:], func=ACT.Copy, scale=GAP_SCALE / FEATS, bias=GAP_SCALE * 1e-6
+            )
+
+        def recip_curv(n):
+            live["recip", n] = column("recip")
+            nc.vector.reciprocal(out=live["recip", n][:], in_=live["curv", n][:])
 
         def ratio(n):
-            a = pool.tile([P, 1], F32, name="gam_a", tag="gam_a", bufs=4)
-            nc.scalar.activation(out=a[:], in_=st["gsum", n][:], func=ACT.Relu, scale=st["rden", n][:])
-            st["gam_a", n] = a
+            if n < TILES - 2:
+                live["ratio", n] = column("ratio")
+                nc.scalar.activation(out=live["ratio", n][:], in_=live["gap", n][:], func=ACT.Relu, scale=live["recip", n][:])
+            else:
+                low = column("low")
+                live["gamma", n] = column("gamma_v")
+                nc.vector.tensor_scalar(out=low[:], in0=live["gap", n][:], scalar1=0.0, scalar2=None, op0=ALU.min)
+                nc.vector.tensor_scalar(
+                    out=live["gamma", n][:], in0=low[:], scalar1=live["recip", n][:], scalar2=1.0, op0=ALU.mult, op1=ALU.min
+                )
 
         def clip(n):
-            b = pool.tile([P, 1], F32, name="gam_b", tag="gam_b", bufs=4)
-            nc.scalar.activation(out=b[:], in_=st["gam_a", n][:], func=ACT.Relu, scale=-1.0, bias=1.0)
-            st["gam_b", n] = b
+            if n < TILES - 2:
+                live["rest", n] = column("rest")
+                nc.scalar.activation(out=live["rest", n][:], in_=live["ratio", n][:], func=ACT.Relu, scale=-1.0, bias=1.0)
 
         def step(n):
-            c = pool.tile([P, 1], F32, name="gam_c", tag="gam_c", bufs=4)
-            nc.scalar.activation(out=c[:], in_=st["gam_b", n][:], func=ACT.Copy, scale=-1.0, bias=1.0)
-            st["gam", n] = c
+            if n < TILES - 2:
+                live["gamma", n] = column("gamma")
+                nc.scalar.activation(out=live["gamma", n][:], in_=live["rest", n][:], func=ACT.Copy, scale=-1.0, bias=1.0)
 
         def scale_step(n):
-            rt = st["r", n // GROUP][:, n % GROUP, :]
-            if n < NT - VFIN:
-                t = pool.tile([P, FEATS], F32, name="ge", tag="ge", bufs=4)
-                nc.scalar.activation(out=t[:], in_=st["e", n][:], func=ACT.Copy, scale=st["gam", n][:])
-                st["ge", n] = t
+            if n < TILES - VECTOR_TAIL:
+                if ("ge", n // 2) not in live:
+                    live["ge", n // 2] = work.tile([P, 2, FEATS], F32, name="ge", tag="ge", bufs=3)
+                nc.scalar.activation(out=live["ge", n // 2][:, n % 2], in_=live["e", n][:], func=ACT.Copy, scale=live["gamma", n][:])
             else:
-                o = pool.tile([P, FEATS], F32, name="o_sb", tag="o_sb", bufs=4)
-                nc.vector.scalar_tensor_tensor(out=o[:], in0=st["e", n][:], scalar=st["gam", n][:], in1=rt, op0=ALU.mult, op1=ALU.add)
-                nc.sync.dma_start(out=out_hbm[n // GROUP][:, n % GROUP, :], in_=o[:])
+                tile = work.tile([P, FEATS], F32, name="out_tile", tag="out_tile", bufs=4)
+                nc.vector.scalar_tensor_tensor(
+                    out=tile[:], in0=live["e", n][:], scalar=live["gamma", n][:], in1=rows_of("r", n), op0=ALU.mult, op1=ALU.add
+                )
+                nc.sync.dma_start(out=out_hbm[n // GROUP][:, n % GROUP, :], in_=tile[:])
 
         def finish(n):
-            if n < NT - VFIN:
-                t = pool.tile([P, FEATS], F32, name="o_sb", tag="o_sb", bufs=4)
-                nc.gpsimd.tensor_tensor(out=t[:], in0=st["ge", n][:], in1=st["r", n // GROUP][:, n % GROUP, :], op=ALU.add)
-                nc.sync.dma_start(out=out_hbm[n // GROUP][:, n % GROUP, :], in_=t[:])
+            if n < TILES - VECTOR_TAIL:
+                i = slice(n % GROUP - 1, n % GROUP + 1)
+                tile = work.tile([P, 2, FEATS], F32, name="out_pair", tag="out_pair", bufs=3)
+                nc.gpsimd.tensor_tensor(out=tile[:], in0=live["ge", n // 2][:], in1=live["r", n // GROUP][:, i, :], op=ALU.add)
+                nc.sync.dma_start(out=out_hbm[n // GROUP][:, i, :], in_=tile[:])
 
-        def widen(q):
-            h = slice(q * HALF, (q + 1) * HALF)
-            for t in (2, 3):
-                nc.scalar.activation(out=enc_wide[q][:, t, :], in_=enc_u8[:, t, h].bitcast(FP8), func=ACT.Copy, scale=enc_s[:, t : t + 1])
-            for t in (0, 1):
-                nc.vector.tensor_scalar(out=enc_wide[q][:, t, :], in0=enc_u8[:, t, h].bitcast(FP8), scalar1=enc_s[:, t : t + 1], scalar2=None, op0=ALU.mult)
-
-        def enc_interleave(q):
-            src = enc_wide[q][:].rearrange("p t (c u) -> p u c t", u=4)
-            if q == 0:
-                nc.vector.tensor_copy(out=enc_grp[q][:], in_=src)
-            else:
-                for v in (0, 2):
-                    nc.scalar.copy(out=enc_grp[q][:, v : v + 2], in_=src[:, v : v + 2])
-
-        def enc_quant(q):
-            nc.vector.quantize_mx(out=enc_codes[q][:].bitcast(FP8X4), scales=enc_scales[q][:], in_=enc_grp[q][:].rearrange("p u c t -> p (u c t)"))
-
-        def dec_piece(i):
-            q, m = i // 2, slice((i % 2) * 256, (i % 2 + 1) * 256)
-            nc.vector.tensor_copy(out=dec_grp[:, q, m, :], in_=dec_raw[:, q, :, m].rearrange("p t m -> p m t"))
-
-        def dec_quant(q):
-            nc.vector.quantize_mx(out=dec_codes[:, q, :].bitcast(FP8X4), scales=dec_scales[:, q, :], in_=dec_grp[:, q].rearrange("p m t -> p (m t)"))
-
-        nc.sync.dma_start(out=enc_u8[:], in_=enc_bytes.rearrange("(p t) k -> p t k", t=4))
-        nc.scalar.dma_start(out=enc_s[:], in_=enc_scale.rearrange("(p t) o -> p (t o)", t=4))
-        nc.scalar.dma_start(out=p_sb[:], in_=p.rearrange("(p t) -> p t", t=4))
-        nc.scalar.dma_start(out=g_sb[:], in_=g.rearrange("(q p t) -> p q t", p=P, t=4))
-        load_r(0)
-        load_z(0)
-        nc.sync.dma_start(out=dec_raw[:], in_=dec.rearrange("(q p t) m -> p q t m", p=P, t=4))
-        load_r(1)
-        load_z(1)
-        load_r(2)
-        nc.vector.memset(warm[:], 0.0)
-        nc.scalar.activation(out=warm[:, 1:2], in_=warm[:, 0:1], func=ACT.Exp)
-        make_identity(nc, ident[:])
-
-        stages = {
-            "r_transpose": r_transpose, "r_gain": r_gain, "r_quant": r_quant, "grad": grad, "row_min": row_min, "exponent": exponent,
-            "total_a": total_a, "total_b": total_b, "recip_total": recip_total, "normalise": normalise, "subtract": subtract, "gap": gap,
-            "d_transpose": d_transpose, "d_gain": d_gain, "d_quant": d_quant, "decode": decode, "square": square, "curvature": curvature,
-            "recip_curv": recip_curv, "gap_sum": gap_sum, "ratio": ratio, "clip": clip, "step": step,
-            "scale_step": scale_step, "finish": finish,
+        by_pair = (r_transpose, r_gain, r_quantise, d_quantise)
+        plan = (
+            (step, -5), (normalise, -1, 1), (gap_sum, -4), (gap_sum, -3), (row_min, 0, 0), (grad, 0, 1),
+            (scale_step, -5), (d_gain, -2, 0), (decode, -4), (subtract, -1, 1), (row_min, 0, 1), (gap, -1, 0),
+            (d_transpose, -1, 0), (exponent, 0, 0), (finish, -5), (d_gain, -2, 1), (exponent, 0, 1), (grad, 1, 0),
+            (gap, -1, 1), (decode, -3), (total_a, 0), (total_b, 0), (square, -4), (recip_total, 0), (row_min, 1, 0),
+            (grad, 1, 1), (normalise, 0, 0), (r_transpose, 2), (d_gain, -1, 0), (curvature, -4), (normalise, 0, 1),
+            (subtract, 0, 0), (row_min, 1, 1), (d_transpose, -1, 1), (square, -3), (recip_curv, -4), (r_gain, 2),
+            (exponent, 1, 0), (subtract, 0, 1), (d_gain, -1, 1), (d_transpose, 0, 0), (exponent, 1, 1), (gap, 0, 0),
+            (total_a, 1), (ratio, -4), (curvature, -3), (total_b, 1), (clip, -4), (recip_curv, -3), (recip_total, 1),
+            (step, -4), (grad, 2, 0), (d_quantise, -1), (ratio, -3), (normalise, 1, 0), (r_quantise, 2),
+            (d_transpose, 0, 1), (clip, -3), (scale_step, -4), (gap, 0, 1), (subtract, 1, 0),
+        )
+        fill = {
+            (gap, -1, 0): lambda: dec_interleave(1, 0),
+            (gap, -1, 1): lambda: dec_interleave(1, 1),
+            (d_gain, -1, 0): lambda: dec_quantise(0),
+            (d_gain, -1, 1): lambda: dec_quantise(1),
         }
-        by_pair = {"r_transpose", "r_gain", "r_quant", "d_quant"}
 
         def period(k):
             if k > 0 and k % 2 == 0:
-                if k // 2 + 2 < NGROUP:
+                if k // 2 + 2 < GROUPS:
                     load_r(k // 2 + 2)
-                if k // 2 + 1 < NGROUP:
+                if k // 2 + 1 < GROUPS:
                     load_z(k // 2 + 1)
-            for name, off, q in PLAN:
-                if name in by_pair:
-                    if 0 <= k + off < NPAIR:
-                        stages[name](k + off)
-                    n = k + off
-                else:
-                    n = 2 * k + off
-                    if 0 <= n < NT:
-                        if q is None:
-                            stages[name](n)
-                        else:
-                            stages[name](n, q)
-                for task in FILL.get((name, n, q), ()):
-                    task()
+            for stage, shift, *half in plan:
+                index, count = (k + shift, PAIRS) if stage in by_pair else (2 * k + shift, TILES)
+                if 0 <= index < count:
+                    stage(index, *half)
+                elif (stage, index, *half) in fill:
+                    fill[(stage, index, *half)]()
 
-        FILL = {
-            ("gap", -1, 0): [lambda: dec_piece(0)],
-            ("gap", -1, 1): [lambda: dec_piece(1)],
-            ("d_gain", -1, 0): [lambda: dec_piece(2)],
-            ("d_gain", -1, 1): [lambda: dec_piece(3)],
-            ("d_quant", -1, None): [lambda: dec_quant(0), lambda: dec_quant(1)],
-        }
-        widen(0)
-        widen(1)
+        nc.sync.dma_start(out=enc_u8[:], in_=enc_bytes.rearrange("(w t) k -> w t k", t=PACK))
+        nc.scalar.dma_start(out=enc_s[:], in_=enc_scale.rearrange("(w t) o -> w (t o)", t=PACK))
+        nc.scalar.dma_start(out=p_sb[:], in_=p.rearrange("(w t) -> w t", t=PACK))
+        nc.scalar.dma_start(out=g_sb[:], in_=g.rearrange("(q w t) -> w q t", w=P, t=PACK))
+        load_r(0, parts=2)
+        nc.sync.dma_start(out=dec_raw[:], in_=dec.rearrange("(q w t) f -> w q t f", w=P, t=PACK))
+        load_z(0)
+        load_r(1)
+        load_z(1)
+        load_r(2)
+        nc.vector.memset(table[:], 0.0)
+        nc.scalar.activation(out=table[:, 1:2], in_=table[:, 0:1], func=ACT.Exp)
+        make_identity(nc, identity[:])
+
+        enc_widen(0)
+        enc_widen(1)
         r_transpose(0)
         r_transpose(1)
         enc_interleave(0)
         enc_interleave(1)
+        dec_interleave(0, 0)
+        dec_interleave(0, 1)
         r_gain(0)
-        enc_quant(0)
-        r_quant(0)
+        enc_quantise(0)
+        r_quantise(0)
         grad(0, 0)
         r_gain(1)
-        enc_quant(1)
-        r_quant(1)
-        for k in range(NPAIR + 6):
+        enc_quantise(1)
+        r_quantise(1)
+
+        for k in range(PAIRS + 3):
             period(k)

import math
from contextlib import ExitStack

import concourse.mybir as mybir
from concourse.masks import make_identity

ROWS, CODES, FEATS = 4096, 1024, 512
RADIUS = 64.0
FLOPS = 2 * 2 * ROWS * CODES * FEATS

F32 = mybir.dt.float32
BF16 = mybir.dt.bfloat16
U32 = mybir.dt.uint32
U8 = mybir.dt.uint8
FP8 = mybir.dt.float8_e4m3fn
FP8X4 = mybir.dt.float8_e4m3fn_x4
ALU = mybir.AluOpType
ACT = mybir.ActivationFunctionType

P = 128
PACK = 4
HALF = 512
GROUP = 4
TILES = ROWS // P
PAIRS = TILES // 2
GROUPS = TILES // GROUP
VECTOR_TAIL = 6
STATS = 8

GAP_SCALE = -math.sqrt(FEATS * CODES)


def tile_smoothedfrankwolfesimplexcoding_t_kernel(tc, r, z, p, enc_bytes, enc_scale, g, dec, out):
    nc = tc.nc
    r_hbm = r.rearrange("(m w j) f -> m w j f", w=P, j=GROUP)
    z_hbm = z.rearrange("(m w j) k -> m w j k", w=P, j=GROUP)
    out_hbm = out.rearrange("(m w j) f -> m w j f", w=P, j=GROUP)

    with ExitStack() as ctx:
        keep = ctx.enter_context(tc.tile_pool(name="keep", bufs=1))
        work = ctx.enter_context(tc.tile_pool(name="work", bufs=2))
        psum = ctx.enter_context(tc.psum_pool(name="psum", bufs=2))
        ctx.enter_context(tc.manual_schedule())

        identity = keep.tile([P, P], F32, name="identity")
        table = keep.tile([P, 2], F32, name="table")
        p_sb = keep.tile([P, PACK], BF16, name="p_sb")
        g_sb = keep.tile([P, 2, PACK], BF16, name="g_sb")
        enc_u8 = keep.tile([P, PACK, CODES], U8, name="enc_u8", align_bytes=64)
        enc_s = keep.tile([P, PACK], F32, name="enc_s")
        dec_raw = keep.tile([P, 2, PACK, FEATS], BF16, name="dec_raw", align_bytes=64)
        enc_wide, enc_words, enc_codes, enc_scales, dec_words, dec_codes, dec_scales = [], [], [], [], [], [], []
        for q in range(2):
            wide = keep.tile([P, PACK, HALF], BF16, name=f"enc_wide{q}", align_bytes=64)
            words = keep.tile([P, PACK, P, PACK], BF16, name=f"enc_words{q}", align_bytes=64)
            codes = keep.tile([P, HALF], U32, name=f"enc_codes{q}", align_bytes=64)
            scales = keep.tile([P, HALF], U8, name=f"enc_scales{q}", align_bytes=64)
            enc_wide.append(wide)
            enc_words.append(words)
            enc_codes.append(codes)
            enc_scales.append(scales)
            words = keep.tile([P, FEATS, PACK], BF16, name=f"dec_words{q}", align_bytes=64)
            codes = keep.tile([P, FEATS], U32, name=f"dec_codes{q}", align_bytes=64)
            scales = keep.tile([P, FEATS], U8, name=f"dec_scales{q}", align_bytes=64)
            dec_words.append(words)
            dec_codes.append(codes)
            dec_scales.append(scales)

        live = {}

        def column(name):
            return work.tile([P, 1], F32, name=name, tag=name, bufs=STATS)


        def load_r(m, parts=1):
            tile = work.tile([P, GROUP, FEATS], BF16, name="r_sb", tag="r_sb", bufs=6, align_bytes=64)
            width = GROUP // parts
            for j in range(0, GROUP, width):
                nc.sync.dma_start(out=tile[:, j : j + width], in_=r_hbm[m][:, j : j + width])
            live["r", m] = tile

        def load_z(m):
            tile = work.tile([P, GROUP, CODES], BF16, name="z_sb", tag="z_sb", bufs=3, align_bytes=64)
            nc.sync.dma_start(out=tile[:], in_=z_hbm[m])
            live["z", m] = tile

        def rows_of(name, n):
            return live[name, n // GROUP][:, n % GROUP, :]


        def enc_widen(q):
            for t in range(PACK):
                plane = enc_u8[:, t, q * HALF : (q + 1) * HALF].bitcast(FP8)
                if t >= (3 if q == 0 else 2):
                    nc.scalar.activation(out=enc_wide[q][:, t, :], in_=plane, func=ACT.Copy, scale=enc_s[:, t : t + 1])
                else:
                    nc.vector.tensor_scalar(
                        out=enc_wide[q][:, t, :], in0=plane, scalar1=enc_s[:, t : t + 1], scalar2=None, op0=ALU.mult
                    )

        def enc_interleave(q):
            source = enc_wide[q][:].rearrange("w t (c u) -> w u c t", u=PACK)
            if q == 0:
                nc.vector.tensor_copy(out=enc_words[q][:], in_=source)
            else:
                for u in (0, 2):
                    nc.scalar.copy(out=enc_words[q][:, u : u + 2], in_=source[:, u : u + 2])

        def enc_quantise(q):
            nc.vector.quantize_mx(
                out=enc_codes[q][:].bitcast(FP8X4), scales=enc_scales[q][:],
                in_=enc_words[q][:].rearrange("w u c t -> w (u c t)"),
            )

        def dec_interleave(q, part):
            f = slice(part * FEATS // 2, (part + 1) * FEATS // 2)
            source = dec_raw[:, q, :, f].rearrange("w t f -> w f t")
            if q == 0:
                nc.scalar.copy(out=dec_words[q][:, f, :], in_=source)
            else:
                nc.vector.tensor_copy(out=dec_words[q][:, f, :], in_=source)

        def dec_quantise(q):
            nc.vector.quantize_mx(
                out=dec_codes[q][:].bitcast(FP8X4), scales=dec_scales[q][:],
                in_=dec_words[q][:].rearrange("w f t -> w (f t)"),
            )


        def r_transpose(j):
            bank = psum.tile([P, 2, 2 * P], F32, name="turned", tag="turned", bufs=2)
            for i in range(2):
                words = rows_of("r", 2 * j + i).bitcast(F32)
                for u in range(2):
                    nc.tensor.transpose(bank[:, u, i * P : (i + 1) * P], words[:, u : 2 * P : 2], identity[:])
            live["r_turned", j] = bank

        def r_gain(j):
            tile = work.tile([P, 2 * P * PACK], BF16, name="rp", tag="rp", bufs=2, align_bytes=64)
            nc.vector.tensor_tensor(
                out=tile[:].rearrange("w (n u e) -> w n u e", u=2, e=2),
                in0=live["r_turned", j][:].bitcast(BF16).rearrange("w u (n e) -> w n u e", e=2),
                in1=p_sb[:].unsqueeze(1).broadcast_to([P, 2 * P, PACK]).rearrange("w n (u e) -> w n u e", e=2),
                op=ALU.mult,
            )
            live["rp", j] = tile

        def r_quantise(j):
            codes = work.tile([P, 2 * P], U32, name="rp_codes", tag="rp_codes", bufs=4, align_bytes=64)
            scales = work.tile([P, 2 * P], U8, name="rp_scales", tag="rp_scales", bufs=4, align_bytes=64)
            nc.vector.quantize_mx(out=codes[:].bitcast(FP8X4), scales=scales[:], in_=live["rp", j][:])
            live["rp_mx", j] = codes, scales


        def grad(n, q):
            codes, scales = live["rp_mx", n // 2]
            rows = slice(n % 2 * P, (n % 2 + 1) * P)
            bank = psum.tile([P, HALF], F32, name="grad", tag="grad", bufs=4)
            nc.tensor.matmul_mx(
                out=bank[:], lhsT=codes[:, rows].bitcast(FP8X4), lhsT_scale=scales[:, rows],
                rhs=enc_codes[q][:].bitcast(FP8X4), rhs_scale=enc_scales[q][:], start=True, stop=True,
            )
            live["grad", n, q] = bank

        def row_min(n, q):
            unused = work.tile([P, HALF], F32, name="unused", tag="unused", bufs=4)
            least = column("least")
            nc.vector.tensor_scalar(
                out=unused[:], in0=live["grad", n, q][:], scalar1=2.0, scalar2=None if q == 0 else live["least", n][:],
                op0=ALU.mult, op1=ALU.min, accum_out=least[:],
            )
            live["least", n] = least

        def exponent(n, q):
            if q == 0:
                live["s", n] = work.tile([P, 2, PACK, P], F32, name="s_sb", tag="s_sb", bufs=4)
                live["sums", n] = work.tile([P, 2], F32, name="sums", tag="sums", bufs=STATS)
            nc.scalar.activation(
                out=live["s", n][:, q].rearrange("n u c -> n (u c)"), in_=live["grad", n, q][:], func=ACT.Exp,
                scale=-2.0, bias=live["least", n][:], accum_out=live["sums", n][:, q : q + 1],
            )

        def total_a(n):
            live["sum_a", n] = column("sum_a")
            nc.scalar.activation(out=live["sum_a", n][:], in_=live["sums", n][:, 0:1], func=ACT.Copy, scale=1.0 / RADIUS)

        def total_b(n):
            live["sum_b", n] = column("sum_b")
            nc.scalar.activation(
                out=live["sum_b", n][:], in_=live["sums", n][:, 1:2], func=ACT.Identity,
                scale=1.0 / RADIUS, bias=live["sum_a", n][:],
            )

        def recip_total(n):
            live["coef", n] = column("coef")
            nc.vector.reciprocal(out=live["coef", n][:], in_=live["sum_b", n][:])

        def normalise(n, q):
            half = live["s", n][:, q].rearrange("n u c -> n (u c)")
            nc.scalar.activation(out=half, in_=half, func=ACT.Copy, scale=live["coef", n][:])

        def subtract(n, q):
            if q == 0:
                live["d", n] = work.tile([P, 2, PACK, P], F32, name="d_sb", tag="d_sb", bufs=4)
            z_half = rows_of("z", n)[:, q * HALF : (q + 1) * HALF].rearrange("n (c u) -> n u c", u=PACK)
            nc.gpsimd.tensor_tensor(out=live["d", n][:, q], in0=live["s", n][:, q], in1=z_half, op=ALU.subtract)

        def gap(n, q):
            if q == 0:
                live["gaps", n] = work.tile([P, 2], F32, name="gaps", tag="gaps", bufs=STATS)
            unused = work.tile([P, HALF], F32, name="unused", tag="unused", bufs=4)
            nc.vector.scalar_tensor_tensor(
                out=unused[:], in0=live["grad", n, q][:], scalar=1.0, in1=live["d", n][:, q].rearrange("n u c -> n (u c)"),
                op0=ALU.mult, op1=ALU.mult, accum_out=live["gaps", n][:, q : q + 1],
            )

        def gap_sum(n):
            live["gap", n] = column("gap")
            nc.vector.tensor_reduce(out=live["gap", n][:], in_=live["gaps", n][:], axis=mybir.AxisListType.X, op=ALU.add)


        def d_transpose(n, q):
            bank = psum.tile([P, PACK, P], F32, name="turned", tag="turned", bufs=2)
            for u in range(PACK):
                nc.tensor.transpose(bank[:, u, :], live["d", n][:, q, u, :], identity[:])
            live["d_turned", n, q] = bank

        def d_gain(n, q):
            if ("dg", n // 2) not in live:
                live["dg", n // 2] = work.tile([P, 2, 2, P, PACK], BF16, name="dg", tag="dg", bufs=2, align_bytes=64)
            nc.vector.tensor_tensor(
                out=live["dg", n // 2][:, n % 2, q], in0=live["d_turned", n, q][:].rearrange("w t n -> w n t"),
                in1=g_sb[:, q, :].unsqueeze(1).broadcast_to([P, P, PACK]), op=ALU.mult,
            )
            if n == TILES - 2 and q == 1:
                quantise_tiles(n, 1)

        def quantise_tiles(n, count):
            j = n // 2
            if ("dg_mx", j) not in live:
                codes = work.tile([P, 2, 2 * P], U32, name="dg_codes", tag="dg_codes", bufs=2, align_bytes=64)
                scales = work.tile([P, 2, 2 * P], U8, name="dg_scales", tag="dg_scales", bufs=2, align_bytes=64)
                live["dg_mx", j] = codes, scales
            codes, scales = live["dg_mx", j]
            i = slice(n % 2, n % 2 + count)
            nc.vector.quantize_mx(
                out=codes[:, i].rearrange("w i n -> w (i n)").bitcast(FP8X4), scales=scales[:, i].rearrange("w i n -> w (i n)"),
                in_=live["dg", j][:, i].rearrange("w i q n t -> w (i q n t)"),
            )

        def d_quantise(j):
            if j < PAIRS - 1:
                quantise_tiles(2 * j, 2)
            else:
                quantise_tiles(2 * j + 1, 1)

        def decode(n):
            codes, scales = live["dg_mx", n // 2]
            tag, bufs = ("decoded", 2) if n < TILES - 2 else ("grad", 4)
            bank = psum.tile([P, FEATS], F32, name="decoded", tag=tag, bufs=bufs)
            for q in range(2):
                rows = slice(q * P, (q + 1) * P)
                nc.tensor.matmul_mx(
                    out=bank[:], lhsT=codes[:, n % 2, rows].bitcast(FP8X4), lhsT_scale=scales[:, n % 2, rows],
                    rhs=dec_codes[q][:].bitcast(FP8X4), rhs_scale=dec_scales[q][:], start=(q == 0), stop=(q == 1),
                )
            live["e", n] = bank


        def square(n):
            unused = work.tile([P, FEATS], BF16, name="squares", tag="squares", bufs=2)
            live["e_sq", n] = column("e_sq")
            nc.scalar.activation(out=unused[:], in_=live["e", n][:], func=ACT.Square, accum_out=live["e_sq", n][:])

        def curvature(n):
            live["curv", n] = column("curv")
            nc.scalar.activation(
                out=live["curv", n][:], in_=live["e_sq", n][:], func=ACT.Copy, scale=GAP_SCALE / FEATS, bias=GAP_SCALE * 1e-6
            )

        def recip_curv(n):
            live["recip", n] = column("recip")
            nc.vector.reciprocal(out=live["recip", n][:], in_=live["curv", n][:])

        def ratio(n):
            if n < TILES - 2:
                live["ratio", n] = column("ratio")
                nc.scalar.activation(out=live["ratio", n][:], in_=live["gap", n][:], func=ACT.Relu, scale=live["recip", n][:])
            else:
                low = column("low")
                live["gamma", n] = column("gamma_v")
                nc.vector.tensor_scalar(out=low[:], in0=live["gap", n][:], scalar1=0.0, scalar2=None, op0=ALU.min)
                nc.vector.tensor_scalar(
                    out=live["gamma", n][:], in0=low[:], scalar1=live["recip", n][:], scalar2=1.0, op0=ALU.mult, op1=ALU.min
                )

        def clip(n):
            if n < TILES - 2:
                live["rest", n] = column("rest")
                nc.scalar.activation(out=live["rest", n][:], in_=live["ratio", n][:], func=ACT.Relu, scale=-1.0, bias=1.0)

        def step(n):
            if n < TILES - 2:
                live["gamma", n] = column("gamma")
                nc.scalar.activation(out=live["gamma", n][:], in_=live["rest", n][:], func=ACT.Copy, scale=-1.0, bias=1.0)

        def scale_step(n):
            if n < TILES - VECTOR_TAIL:
                if ("ge", n // 2) not in live:
                    live["ge", n // 2] = work.tile([P, 2, FEATS], F32, name="ge", tag="ge", bufs=3)
                nc.scalar.activation(out=live["ge", n // 2][:, n % 2], in_=live["e", n][:], func=ACT.Copy, scale=live["gamma", n][:])
            else:
                tile = work.tile([P, FEATS], F32, name="out_tile", tag="out_tile", bufs=4)
                nc.vector.scalar_tensor_tensor(
                    out=tile[:], in0=live["e", n][:], scalar=live["gamma", n][:], in1=rows_of("r", n), op0=ALU.mult, op1=ALU.add
                )
                nc.sync.dma_start(out=out_hbm[n // GROUP][:, n % GROUP, :], in_=tile[:])

        def finish(n):
            if n < TILES - VECTOR_TAIL:
                i = slice(n % GROUP - 1, n % GROUP + 1)
                tile = work.tile([P, 2, FEATS], F32, name="out_pair", tag="out_pair", bufs=3)
                nc.gpsimd.tensor_tensor(out=tile[:], in0=live["ge", n // 2][:], in1=live["r", n // GROUP][:, i, :], op=ALU.add)
                nc.sync.dma_start(out=out_hbm[n // GROUP][:, i, :], in_=tile[:])

        by_pair = (r_transpose, r_gain, r_quantise, d_quantise)
        plan = (
            (step, -5), (normalise, -1, 1), (gap_sum, -4), (gap_sum, -3), (row_min, 0, 0), (grad, 0, 1),
            (scale_step, -5), (d_gain, -2, 0), (decode, -4), (subtract, -1, 1), (row_min, 0, 1), (gap, -1, 0),
            (d_transpose, -1, 0), (exponent, 0, 0), (finish, -5), (d_gain, -2, 1), (exponent, 0, 1), (grad, 1, 0),
            (gap, -1, 1), (decode, -3), (total_a, 0), (total_b, 0), (square, -4), (recip_total, 0), (row_min, 1, 0),
            (grad, 1, 1), (normalise, 0, 0), (r_transpose, 2), (d_gain, -1, 0), (curvature, -4), (normalise, 0, 1),
            (subtract, 0, 0), (row_min, 1, 1), (d_transpose, -1, 1), (square, -3), (recip_curv, -4), (r_gain, 2),
            (exponent, 1, 0), (subtract, 0, 1), (d_gain, -1, 1), (d_transpose, 0, 0), (exponent, 1, 1), (gap, 0, 0),
            (total_a, 1), (ratio, -4), (curvature, -3), (total_b, 1), (clip, -4), (recip_curv, -3), (recip_total, 1),
            (step, -4), (grad, 2, 0), (d_quantise, -1), (ratio, -3), (normalise, 1, 0), (r_quantise, 2),
            (d_transpose, 0, 1), (clip, -3), (scale_step, -4), (gap, 0, 1), (subtract, 1, 0),
        )
        fill = {
            (gap, -1, 0): lambda: dec_interleave(1, 0),
            (gap, -1, 1): lambda: dec_interleave(1, 1),
            (d_gain, -1, 0): lambda: dec_quantise(0),
            (d_gain, -1, 1): lambda: dec_quantise(1),
        }

        def period(k):
            if k > 0 and k % 2 == 0:
                if k // 2 + 2 < GROUPS:
                    load_r(k // 2 + 2)
                if k // 2 + 1 < GROUPS:
                    load_z(k // 2 + 1)
            for stage, shift, *half in plan:
                index, count = (k + shift, PAIRS) if stage in by_pair else (2 * k + shift, TILES)
                if 0 <= index < count:
                    stage(index, *half)
                elif (stage, index, *half) in fill:
                    fill[(stage, index, *half)]()

        nc.sync.dma_start(out=enc_u8[:], in_=enc_bytes.rearrange("(w t) k -> w t k", t=PACK))
        nc.scalar.dma_start(out=enc_s[:], in_=enc_scale.rearrange("(w t) o -> w (t o)", t=PACK))
        nc.scalar.dma_start(out=p_sb[:], in_=p.rearrange("(w t) -> w t", t=PACK))
        nc.scalar.dma_start(out=g_sb[:], in_=g.rearrange("(q w t) -> w q t", w=P, t=PACK))
        load_r(0, parts=2)
        nc.sync.dma_start(out=dec_raw[:], in_=dec.rearrange("(q w t) f -> w q t f", w=P, t=PACK))
        load_z(0)
        load_r(1)
        load_z(1)
        load_r(2)
        nc.vector.memset(table[:], 0.0)
        nc.scalar.activation(out=table[:, 1:2], in_=table[:, 0:1], func=ACT.Exp)
        make_identity(nc, identity[:])

        enc_widen(0)
        enc_widen(1)
        r_transpose(0)
        r_transpose(1)
        enc_interleave(0)
        enc_interleave(1)
        dec_interleave(0, 0)
        dec_interleave(0, 1)
        r_gain(0)
        enc_quantise(0)
        r_quantise(0)
        grad(0, 0)
        r_gain(1)
        enc_quantise(1)
        r_quantise(1)

        for k in range(PAIRS + 3):
            period(k)
